import numpy as np
import ml_dtypes


def mxq(x, axis, fmt="e4m3"):
    dtype, down = {"e4m3": (ml_dtypes.float8_e4m3fn, 7), "e5m2": (ml_dtypes.float8_e5m2, 14)}[fmt]
    v = np.moveaxis(np.asarray(x, np.float32).astype(ml_dtypes.bfloat16).astype(np.float64), axis, -1)
    blocks = v.reshape(v.shape[:-1] + (-1, 32))
    amax = np.abs(blocks).max(-1, keepdims=True)
    byte = np.maximum(np.where(amax > 0, np.frexp(amax)[1] - 1 + 127, 0) - down, 1)
    scale = np.exp2(byte - 127.0)
    codes = (blocks / scale).astype(np.float32).astype(dtype).astype(np.float64)
    return np.moveaxis((codes * scale).reshape(v.shape), -1, axis)


WIDE = False


def mx_kscale(k):
    if not WIDE:
        return np.ones(k)
    levels = np.array([10, -10, 5, -5, 0])
    if k % 512:
        return np.exp2(np.random.permutation(np.resize(levels, k // 32))).repeat(32)
    a = np.empty((k // 512, 16))
    for p in range(k // 512):
        a[p, :8] = np.random.permutation(np.resize(levels, 8))
        for g in range(8):
            far = levels[np.abs(levels - a[p, g]) >= 10]
            a[p, g + 8] = far[np.random.randint(len(far))]
    return np.exp2(a.ravel()).repeat(32)


def f64(x):
    return np.asarray(x).astype(np.float64)


def striped(idx):
    return np.tile(idx.reshape(-1, 16).T, (8, 1)).astype(np.uint16)


def unstriped(offs):
    return offs[:16].T.reshape(-1).astype(np.int64)


E2M1 = np.array([0.0, 0.5, 1.0, 1.5, 2.0, 3.0, 4.0, 6.0, -0.0, -0.5, -1.0, -1.5, -2.0, -3.0, -4.0, -6.0])


def pack_weight(w, fmt):
    k, n = w.shape
    w = f64(np.asarray(w, np.float32).astype(ml_dtypes.bfloat16)).reshape(k // 32, 32, n)
    amax = np.abs(w).max(1)
    if fmt == "e4m3":
        byte = np.frexp(amax)[1] - 1 + 127 - 7
    else:
        mant, ex = np.frexp(amax / 6.0)
        byte = np.where(mant > 0.5, ex, ex - 1) + 127
    byte = np.clip(np.where(amax > 0, byte, 1), 1, 254)
    scaled = (w * np.exp2(127.0 - byte)[:, None, :]).reshape(k, n).astype(np.float32)
    by_word = np.ascontiguousarray(scaled.reshape(k // 512, 128, 4, n).transpose(0, 1, 3, 2))
    if fmt == "e4m3":
        words = by_word.astype(ml_dtypes.float8_e4m3fn).view(np.uint8)
    else:
        c = by_word.astype(ml_dtypes.float4_e2m1fn).view(np.uint8) & 0xF
        words = (c[..., 0::2] | (c[..., 1::2] << 4)).reshape(k // 512, 128, 2 * n)
    return np.ascontiguousarray(words), np.ascontiguousarray(byte.astype(np.uint8).reshape(k // 512, 16, n))


def unpack_weight(words, scales, fmt):
    g, _, n = scales.shape
    words = np.ascontiguousarray(words).reshape(g, 128, n, -1)
    if fmt == "e4m3":
        vals = words.view(ml_dtypes.float8_e4m3fn).astype(np.float64)
    else:
        nib = np.empty((g, 128, n, 4), np.uint8)
        nib[..., 0::2] = words & 0xF
        nib[..., 1::2] = words >> 4
        vals = E2M1[nib]
    vals = vals * np.repeat(np.exp2(scales.astype(np.float64) - 127.0), 8, axis=1)[..., None]
    return vals.transpose(0, 1, 3, 2).reshape(g * 512, n)


def gelu(v):
    return 0.5 * v * (1.0 + np.tanh(np.sqrt(2.0 / np.pi) * (v + 0.044715 * v**3)))


K, H, T, S, T2, P = 1536, 1024, 4096, 1024, 2048, 512

def setup_inputs():
    n = np.random.standard_normal
    s = mx_kscale(K)[:, None]
    u = mx_kscale(H)[:, None]
    tab_words, tab_scales = pack_weight(n((K, T)) * s, "e4m3")
    rock_words, rock_scales = pack_weight(n((K, H)) / np.sqrt(K) / s * u.T, "e2m1")
    return {
        "tab_words": tab_words, "tab_scales": tab_scales,
        "offs": striped(np.random.permutation(T)[:S]),
        "offs2": striped(np.random.permutation(T2)[:S]),
        "offs3": striped(np.random.permutation(T2)[:P]),
        "rock_words": rock_words, "rock_scales": rock_scales,
        "b1": (0.5 * n(H) * u[:, 0]).astype(np.float32),
        "page0": (n((H, T2)) * u).astype(np.float32),
        "soil": n((H, P)).astype(np.float32),
        "gs": (np.exp(0.3 * n(H)) * u[:, 0]).astype(np.float32),
        "w2": (1.2 * n((H, H)) / np.sqrt(H) / u).astype(np.float32),
    }

def reference(tab_words, tab_scales, offs, offs2, offs3, rock_words, rock_scales,
              b1, page0, soil, gs, w2):
    v = unpack_weight(tab_words, tab_scales, "e4m3")[:, unstriped(offs)]
    w1 = unpack_weight(rock_words, rock_scales, "e2m1")
    h = (w1.T @ v) + f64(b1)[:, None]
    page = f64(page0).copy()
    l2 = unstriped(offs2)
    page[:, l2] = np.maximum(page[:, l2], h)
    ground = f64(soil)
    x = page[:, unstriped(offs3)] + f64(gs)[:, None] * ground
    y = mxq(f64(w2), 0, "e4m3").T @ mxq(x, 0, "e4m3")
    z = y + ground
    return 1.0 / (1.0 + np.exp(-z))

@@ -1,0 +1,275 @@
+from contextlib import ExitStack
+
+import concourse.mybir as mybir
+
+K, H, T, S, T2, M = 1536, 1024, 4096, 1024, 2048, 512
+FLOPS = 2 * K * H * S + 2 * H * H * M
+
+F32 = mybir.dt.float32
+BF16 = mybir.dt.bfloat16
+I32 = mybir.dt.int32
+U32 = mybir.dt.uint32
+U16 = mybir.dt.uint16
+U8 = mybir.dt.uint8
+FP8X4 = mybir.dt.float8_e4m3fn_x4
+FP4X4 = mybir.dt.float4_e2m1fn_x4
+ALU = mybir.AluOpType
+ACT = mybir.ActivationFunctionType
+
+P = 128
+PACK = 4
+K_PASS = P * PACK
+BANK = 512
+PASSES1 = K // K_PASS
+PASSES2 = H // K_PASS
+SLICES = H // P
+HALVES = S // BANK
+LIVE_ROWS = 100
+
+
+def tile_list_tilt_register_scores_kernel(
+    tc, tab_words, tab_scales, offs, offs2, offs3, rock_words, rock_scales, b1, page0, soil, gs, w2, out
+):
+    nc = tc.nc
+    with ExitStack() as ctx:
+        lists = ctx.enter_context(tc.tile_pool(name="lists", bufs=1))
+        keep = ctx.enter_context(tc.tile_pool(name="keep", bufs=1))
+        ring = ctx.enter_context(tc.tile_pool(name="ring", bufs=1))
+        psum = ctx.enter_context(tc.psum_pool(name="psum", bufs=8))
+
+        idx = lists.tile([P, S // 16], U16, name="idx")
+        idx2 = lists.tile([P, S // 16], U16, name="idx2")
+        idx3 = lists.tile([P, M // 16], U16, name="idx3")
+
+        tab_scale_rows = keep.tile([P, T], U8, name="tab_scale_rows", align_bytes=64)
+        rock_scale_rows = keep.tile([P, PASSES1, H], U8, name="rock_scale_rows", align_bytes=64)
+        v_planes = [keep.tile([P, S], U8, name=f"v_plane{a}", align_bytes=64) for a in range(PASSES1)]
+        nc.vector.memset(tab_scale_rows[:].bitcast(I32), 0)
+        nc.vector.memset(rock_scale_rows[:].bitcast(I32), 0)
+        for a in range(1, PASSES1):
+            nc.gpsimd.memset(v_planes[a][:].bitcast(I32), 0)
+
+        def big_tile(shape, dtype, name):
+            return ring.tile(shape, dtype, name=name, tag="big", bufs=3, align_bytes=64)
+
+        def load_table(a):
+            words = big_tile([P, T], U32, f"tab{a}")
+            nc.sync.dma_start(
+                out=words[:].bitcast(I32), in_=tab_words[a].rearrange("p t i -> p (t i)").bitcast(I32)
+            )
+            return words
+
+        def load_page(s):
+            g, t = divmod(s, PACK)
+            page = ring.tile([P, T2], F32, name=f"page{s}", tag="page", bufs=7, align_bytes=64)
+            rows = page0[g * K_PASS : (g + 1) * K_PASS, :].rearrange("(p t) c -> t p c", t=PACK)
+            nc.sync.dma_start(out=page[:], in_=rows[t])
+            return page
+
+        tabs = [load_table(0)]
+        for q in range(4):
+            nc.sync.dma_start(
+                out=tab_scale_rows[32 * q : 32 * q + 4 * PASSES1, :].bitcast(I32),
+                in_=tab_scales[:, 4 * q : 4 * q + 4, :].bitcast(I32),
+            )
+        nc.sync.dma_start(idx[:], offs)
+        rock_raw = keep.tile([P, PASSES1, 2 * H], U8, name="rock_raw", align_bytes=64)
+        nc.sync.dma_start(out=rock_raw[:].bitcast(I32), in_=rock_words.rearrange("a p c -> p a c").bitcast(I32))
+        tabs.append(load_table(1))
+        for q in range(4):
+            nc.sync.dma_start(
+                out=rock_scale_rows[32 * q : 32 * q + 4, :, :].bitcast(I32),
+                in_=rock_scales[:, 4 * q : 4 * q + 4, :].rearrange("a r c -> r a c").bitcast(I32),
+            )
+        tabs.append(load_table(2))
+        bias = keep.tile([P, PASSES2, PACK], F32, name="bias")
+        nc.sync.dma_start(out=bias[:], in_=b1.rearrange("(g p t) -> p g t", p=P, t=PACK))
+        nc.sync.dma_start(idx2[:], offs2)
+        pages = [load_page(0), load_page(1)]
+        nc.sync.dma_start(idx3[:], offs3)
+        gain = keep.tile([P, PASSES2, PACK], F32, name="gain")
+        nc.sync.dma_start(out=gain[:], in_=gs.rearrange("(g p t) -> p g t", p=P, t=PACK))
+
+        nc.vector.tensor_copy(v_planes[0][:], tab_scale_rows[:].indirect(idx[:]))
+        for a in range(1, PASSES1):
+            nc.scalar.dma_start(
+                out=v_planes[a][0:LIVE_ROWS, :].bitcast(I32),
+                in_=v_planes[0][4 * a : 4 * a + LIVE_ROWS, :].bitcast(I32),
+            )
+
+        rock_codes = []
+        rock_planes = []
+        v_words = []
+        for a in range(PASSES1):
+            codes = keep.tile([P, 2 * H], U8, name=f"rock_codes{a}", align_bytes=64)
+            nc.vector.tensor_copy(
+                out=codes[:].bitcast(U16).rearrange("p (g t q) -> p g t q", g=PASSES2, t=PACK),
+                in_=rock_raw[:, a, :].bitcast(U16).rearrange("p (g q t) -> p g t q", g=PASSES2, t=PACK),
+            )
+            rock_codes.append(codes)
+            plane = keep.tile([P, H], U8, name=f"rock_plane{a}", align_bytes=64)
+            nc.vector.tensor_copy(
+                out=plane[:].rearrange("p (g t q) -> p g t q", g=PASSES2, t=PACK),
+                in_=rock_scale_rows[:, a, :].rearrange("p (g q t) -> p g t q", g=PASSES2, t=PACK),
+            )
+            rock_planes.append(plane)
+            picked = []
+            for half in range(HALVES):
+                words = keep.tile([P, BANK], U32, name=f"v_words{a}_{half}", align_bytes=64)
+                cols = slice(half * BANK // 16, (half + 1) * BANK // 16)
+                nc.vector.tensor_copy(words[:], tabs[a][:].indirect(idx[:, cols]))
+                picked.append(words)
+            v_words.append(picked)
+
+        soil_in = []
+        for g in range(PASSES2):
+            tile = keep.tile([P, PACK, M], F32, name=f"soil_in{g}", align_bytes=64)
+            soil_in.append(tile)
+
+        def load_soil_in(g):
+            nc.sync.dma_start(
+                out=soil_in[g][:], in_=soil[g * K_PASS : (g + 1) * K_PASS, :].rearrange("(p t) m -> p t m", t=PACK)
+            )
+            for t in range(PACK):
+                nc.scalar.activation(soil_in[g][:, t, :], soil_in[g][:, t, :], ACT.Copy, scale=gain[:, g, t : t + 1])
+
+        def features(s):
+            g, t = divmod(s, PACK)
+            h = ring.tile([P, S], F32, name=f"h{s}", tag="h", bufs=4, align_bytes=64)
+            for half in range(HALVES):
+                cols = slice(half * BANK, (half + 1) * BANK)
+                acc = psum.tile([P, BANK], F32, name=f"h_acc{s}_{half}", tag="bank")
+                for a in range(PASSES1):
+                    nc.tensor.matmul_mx(
+                        out=acc[:],
+                        lhsT=rock_codes[a][:, 2 * P * s : 2 * P * (s + 1)].bitcast(FP4X4),
+                        lhsT_scale=rock_planes[a][:, P * s : P * (s + 1)],
+                        rhs=v_words[a][half][:].bitcast(FP8X4),
+                        rhs_scale=v_planes[a][:, cols],
+                        start=(a == 0),
+                        stop=(a == PASSES1 - 1),
+                    )
+                nc.scalar.activation(h[:, cols], acc[:], ACT.Identity, bias=bias[:, g, t : t + 1])
+            return h
+
+        def excess(s, h, pieces):
+            rise = ring.tile([P, S], F32, name=f"rise{s}", tag="rise", bufs=3, align_bytes=64)
+            width = S // pieces
+            for i in range(pieces):
+                cols = slice(i * width, (i + 1) * width)
+                entries = idx2[:, i * width // 16 : (i + 1) * width // 16]
+                nc.vector.tensor_tensor(rise[:, cols], pages[s][:].indirect(entries), h[:, cols], ALU.subtract)
+                nc.scalar.activation(rise[:, cols], rise[:, cols], ACT.Relu)
+            return rise
+
+        def interleave(engine_copy, dst, src):
+            engine_copy(
+                out=dst.rearrange("p (c i) t -> p c t i", i=4),
+                in_=src.rearrange("p t (c i) -> p c t i", i=4),
+            )
+
+        w_codes = []
+        w_planes = []
+
+        def quantize_w2(g):
+            raw = big_tile([P, PACK, H], F32, f"w2_raw{g}")
+            nc.sync.dma_start(
+                out=raw[:], in_=w2[g * K_PASS : (g + 1) * K_PASS, :].rearrange("(p t) n -> p t n", t=PACK)
+            )
+            for half in range(H // BANK):
+                woven = ring.tile([P, BANK, PACK], BF16, name=f"w2_woven{g}_{half}", tag="woven", bufs=2, align_bytes=64)
+                interleave(nc.scalar.copy, woven[:], raw[:, :, half * BANK : (half + 1) * BANK])
+                codes = keep.tile([P, BANK], U32, name=f"w_codes{g}_{half}", align_bytes=64)
+                plane = keep.tile([P, BANK], U8, name=f"w_plane{g}_{half}", align_bytes=64)
+                nc.vector.quantize_mx(
+                    out=codes[:].bitcast(FP8X4), scales=plane[:], in_=woven[:].rearrange("p c t -> p (c t)")
+                )
+                w_codes.append(codes)
+                w_planes.append(plane)
+
+        x_rows = []
+
+        def read_page(s, pieces):
+            g, t = divmod(s, PACK)
+            if t == 0:
+                x_rows.append(ring.tile([P, PACK, M], F32, name=f"x_rows{g}", tag="x_rows", bufs=1, align_bytes=64))
+            width = M // pieces
+            for i in range(pieces):
+                cols = slice(i * width, (i + 1) * width)
+                entries = idx3[:, i * width // 16 : (i + 1) * width // 16]
+                nc.vector.tensor_tensor(x_rows[g][:, t, cols], pages[s][:].indirect(entries), soil_in[g][:, t, cols], ALU.add)
+
+        y_acc = []
+        x_codes = []
+        x_planes = []
+
+        def quantize_x(g, copies):
+            woven = keep.tile([P, M, PACK], BF16, name=f"x_woven{g}", align_bytes=64)
+            width = M // len(copies)
+            for i, engine_copy in enumerate(copies):
+                cols = slice(i * width, (i + 1) * width)
+                interleave(engine_copy, woven[:, cols, :], x_rows[g][:, :, cols])
+            codes = keep.tile([P, M], U32, name=f"x_codes{g}", align_bytes=64)
+            plane = keep.tile([P, M], U8, name=f"x_plane{g}", align_bytes=64)
+            nc.vector.quantize_mx(
+                out=codes[:].bitcast(FP8X4), scales=plane[:], in_=woven[:].rearrange("p c t -> p (c t)")
+            )
+            x_codes.append(codes)
+            x_planes.append(plane)
+
+        def second_product(g):
+            for n in range(SLICES):
+                if g == 0:
+                    y_acc.append(psum.tile([P, BANK], F32, name=f"y_acc{n}", tag="bank"))
+                which = g * (H // BANK) + n // PACK
+                cols = slice((n % PACK) * P, (n % PACK + 1) * P)
+                nc.tensor.matmul_mx(
+                    out=y_acc[n][:],
+                    lhsT=w_codes[which][:, cols].bitcast(FP8X4),
+                    lhsT_scale=w_planes[which][:, cols],
+                    rhs=x_codes[g][:].bitcast(FP8X4),
+                    rhs_scale=x_planes[g][:],
+                    start=(g == 0),
+                    stop=(g == PASSES2 - 1),
+                )
+
+        hs = [features(0)]
+        rises = [excess(0, hs[0], HALVES)]
+        hs.append(features(1))
+        rises.append(excess(1, hs[1], 1))
+        soil_out = None
+        for s in range(SLICES):
+            if s + 2 < SLICES:
+                pages.append(load_page(s + 2))
+                hs.append(features(s + 2))
+            if s == 0:
+                load_soil_in(0)
+            if s == 3:
+                quantize_w2(0)
+            if s == 4:
+                load_soil_in(1)
+            if s == 5:
+                quantize_w2(1)
+            if s == 6:
+                soil_out = big_tile([P, SLICES, M], F32, "soil_out")
+                nc.sync.dma_start(out=soil_out[:], in_=soil.rearrange("(n p) m -> p n m", p=P))
+            nc.vector.tensor_tensor(pages[s][:].indirect(idx2[:]), hs[s][:], rises[s][:], ALU.add)
+            if s + 2 < SLICES:
+                rises.append(excess(s + 2, hs[s + 2], 1))
+            if s == SLICES - 1:
+                read_page(s - 1, 1)
+                read_page(s, 2)
+            elif s < SLICES - 2:
+                read_page(s, 1)
+            if s == 3:
+                quantize_x(0, [nc.scalar.copy])
+            if s == 5:
+                second_product(0)
+        quantize_x(1, [nc.scalar.copy, nc.vector.tensor_copy])
+        second_product(1)
+
+        for n in range(SLICES):
+            z = ring.tile([P, M], F32, name=f"z{n}", tag="z", bufs=4, align_bytes=64)
+            nc.vector.tensor_tensor(z[:], y_acc[n][:], soil_out[:, n, :], ALU.add)
+            nc.scalar.activation(z[:], z[:], ACT.Sigmoid)
+            nc.sync.dma_start(out=out[n * P : (n + 1) * P, :], in_=z[:])

@@ -1,6 +1,7 @@
 from contextlib import ExitStack
 
 import concourse.mybir as mybir
+from concourse.masks import make_identity
 
 K, H, T, S, T2, M = 1536, 1024, 4096, 1024, 2048, 512
 FLOPS = 2 * K * H * S + 2 * H * H * M
@@ -35,19 +36,23 @@ def tile_list_tilt_register_scores_kernel(
         lists = ctx.enter_context(tc.tile_pool(name="lists", bufs=1))
         keep = ctx.enter_context(tc.tile_pool(name="keep", bufs=1))
         ring = ctx.enter_context(tc.tile_pool(name="ring", bufs=1))
-        psum = ctx.enter_context(tc.psum_pool(name="psum", bufs=8))
+        psum = ctx.enter_context(tc.psum_pool(name="psum", bufs=1))
 
         idx = lists.tile([P, S // 16], U16, name="idx")
         idx2 = lists.tile([P, S // 16], U16, name="idx2")
         idx3 = lists.tile([P, M // 16], U16, name="idx3")
 
-        tab_scale_rows = keep.tile([P, T], U8, name="tab_scale_rows", align_bytes=64)
-        rock_scale_rows = keep.tile([P, PASSES1, H], U8, name="rock_scale_rows", align_bytes=64)
+        tab_scale_rows = keep.tile([P, T], U8, name="tab_scale_rows", tag="tab_scale_rows", align_bytes=64)
+        rock_scale_rows = keep.tile([P, PASSES1, H], U8, name="rock_scale_rows", tag="rock_scale_rows", align_bytes=64)
         v_planes = [keep.tile([P, S], U8, name=f"v_plane{a}", align_bytes=64) for a in range(PASSES1)]
-        nc.vector.memset(tab_scale_rows[:].bitcast(I32), 0)
+        nc.gpsimd.memset(tab_scale_rows[:].bitcast(I32), 0)
         nc.vector.memset(rock_scale_rows[:].bitcast(I32), 0)
         for a in range(1, PASSES1):
-            nc.gpsimd.memset(v_planes[a][:].bitcast(I32), 0)
+            nc.vector.memset(v_planes[a][:].bitcast(I32), 0)
+        identity = keep.tile([P, P], F32, name="identity", align_bytes=64)
+
+        def bank(name, tag):
+            return psum.tile([P, BANK], F32, name=name, tag=tag, bufs=4 if tag == "h_bank" else 2)
 
         def big_tile(shape, dtype, name):
             return ring.tile(shape, dtype, name=name, tag="big", bufs=3, align_bytes=64)
@@ -61,14 +66,14 @@ def tile_list_tilt_register_scores_kernel(
 
         def load_page(s):
             g, t = divmod(s, PACK)
-            page = ring.tile([P, T2], F32, name=f"page{s}", tag="page", bufs=7, align_bytes=64)
+            page = ring.tile([P, T2], F32, name=f"page{s}", tag="page", bufs=6, align_bytes=64)
             rows = page0[g * K_PASS : (g + 1) * K_PASS, :].rearrange("(p t) c -> t p c", t=PACK)
             nc.sync.dma_start(out=page[:], in_=rows[t])
             return page
 
         tabs = [load_table(0)]
         for q in range(4):
-            nc.sync.dma_start(
+            nc.gpsimd.dma_start(
                 out=tab_scale_rows[32 * q : 32 * q + 4 * PASSES1, :].bitcast(I32),
                 in_=tab_scales[:, 4 * q : 4 * q + 4, :].bitcast(I32),
             )
@@ -77,13 +82,16 @@ def tile_list_tilt_register_scores_kernel(
         nc.sync.dma_start(out=rock_raw[:].bitcast(I32), in_=rock_words.rearrange("a p c -> p a c").bitcast(I32))
         tabs.append(load_table(1))
         for q in range(4):
-            nc.sync.dma_start(
+            nc.gpsimd.dma_start(
                 out=rock_scale_rows[32 * q : 32 * q + 4, :, :].bitcast(I32),
                 in_=rock_scales[:, 4 * q : 4 * q + 4, :].rearrange("a r c -> r a c").bitcast(I32),
             )
+        make_identity(nc, identity[:])
         tabs.append(load_table(2))
         bias = keep.tile([P, PASSES2, PACK], F32, name="bias")
         nc.sync.dma_start(out=bias[:], in_=b1.rearrange("(g p t) -> p g t", p=P, t=PACK))
+        neg_bias = keep.tile([P, PASSES2, PACK], F32, name="neg_bias")
+        nc.scalar.mul(neg_bias[:], bias[:], -1.0)
         nc.sync.dma_start(idx2[:], offs2)
         pages = [load_page(0), load_page(1)]
         nc.sync.dma_start(idx3[:], offs3)
@@ -92,7 +100,7 @@ def tile_list_tilt_register_scores_kernel(
 
         nc.vector.tensor_copy(v_planes[0][:], tab_scale_rows[:].indirect(idx[:]))
         for a in range(1, PASSES1):
-            nc.scalar.dma_start(
+            nc.gpsimd.dma_start(
                 out=v_planes[a][0:LIVE_ROWS, :].bitcast(I32),
                 in_=v_planes[0][4 * a : 4 * a + LIVE_ROWS, :].bitcast(I32),
             )
@@ -115,7 +123,8 @@ def tile_list_tilt_register_scores_kernel(
             rock_planes.append(plane)
             picked = []
             for half in range(HALVES):
-                words = keep.tile([P, BANK], U32, name=f"v_words{a}_{half}", align_bytes=64)
+                tag = "tab_scale_rows" if (a, half) == (0, 1) else "rock_scale_rows" if (a, half) == (2, 0) else f"v_words{a}_{half}"
+                words = keep.tile([P, BANK], U32, name=f"v_words{a}_{half}", tag=tag, align_bytes=64)
                 cols = slice(half * BANK // 16, (half + 1) * BANK // 16)
                 nc.vector.tensor_copy(words[:], tabs[a][:].indirect(idx[:, cols]))
                 picked.append(words)
@@ -138,7 +147,7 @@ def tile_list_tilt_register_scores_kernel(
             h = ring.tile([P, S], F32, name=f"h{s}", tag="h", bufs=4, align_bytes=64)
             for half in range(HALVES):
                 cols = slice(half * BANK, (half + 1) * BANK)
-                acc = psum.tile([P, BANK], F32, name=f"h_acc{s}_{half}", tag="bank")
+                acc = bank(f"h_acc{s}_{half}", "h_bank")
                 for a in range(PASSES1):
                     nc.tensor.matmul_mx(
                         out=acc[:],
@@ -149,17 +158,33 @@ def tile_list_tilt_register_scores_kernel(
                         start=(a == 0),
                         stop=(a == PASSES1 - 1),
                     )
-                nc.scalar.activation(h[:, cols], acc[:], ACT.Identity, bias=bias[:, g, t : t + 1])
+                nc.scalar.activation(h[:, cols], acc[:], ACT.Identity, bias=neg_bias[:, g, t : t + 1], scale=-1.0)
             return h
 
-        def excess(s, h, pieces):
-            rise = ring.tile([P, S], F32, name=f"rise{s}", tag="rise", bufs=3, align_bytes=64)
-            width = S // pieces
-            for i in range(pieces):
-                cols = slice(i * width, (i + 1) * width)
-                entries = idx2[:, i * width // 16 : (i + 1) * width // 16]
-                nc.vector.tensor_tensor(rise[:, cols], pages[s][:].indirect(entries), h[:, cols], ALU.subtract)
-                nc.scalar.activation(rise[:, cols], rise[:, cols], ACT.Relu)
+        def fetch_old(s):
+            old = ring.tile([P, S], F32, name=f"old{s}", tag="old", bufs=4, align_bytes=64)
+            nc.vector.tensor_copy(old[:], pages[s][:].indirect(idx2[:]))
+            return old
+
+        def excess(s, neg_h, old):
+            turned = ring.tile([P, S], F32, name=f"turned{s}", tag="turned", bufs=2, align_bytes=64)
+            rise = ring.tile([P, S], F32, name=f"rise{s}", tag="rise", bufs=2, align_bytes=64)
+            for half in range(HALVES):
+                cols = slice(half * BANK, (half + 1) * BANK)
+                diff = bank(f"diff{s}_{half}", "d_bank")
+                for i in range(BANK // P):
+                    block = slice(half * BANK + i * P, half * BANK + (i + 1) * P)
+                    dst = diff[:, i * P : (i + 1) * P]
+                    nc.tensor.matmul(dst, lhsT=old[:, block], rhs=identity[:], is_transpose=True, start=True, stop=False)
+                    nc.tensor.matmul(dst, lhsT=neg_h[:, block], rhs=identity[:], is_transpose=True, start=False, stop=True)
+                nc.scalar.activation(turned[:, cols], diff[:], ACT.Relu, scale=-1.0)
+            for half in range(HALVES):
+                cols = slice(half * BANK, (half + 1) * BANK)
+                back = bank(f"back{s}_{half}", "r_bank")
+                for i in range(BANK // P):
+                    block = slice(half * BANK + i * P, half * BANK + (i + 1) * P)
+                    nc.tensor.transpose(back[:, i * P : (i + 1) * P], turned[:, block], identity[:])
+                nc.scalar.copy(rise[:, cols], back[:])
             return rise
 
         def interleave(engine_copy, dst, src):
@@ -204,7 +229,7 @@ def tile_list_tilt_register_scores_kernel(
         x_planes = []
 
         def quantize_x(g, copies):
-            woven = keep.tile([P, M, PACK], BF16, name=f"x_woven{g}", align_bytes=64)
+            woven = ring.tile([P, M, PACK], BF16, name=f"x_woven{g}", tag="woven", bufs=2, align_bytes=64)
             width = M // len(copies)
             for i, engine_copy in enumerate(copies):
                 cols = slice(i * width, (i + 1) * width)
@@ -220,7 +245,7 @@ def tile_list_tilt_register_scores_kernel(
         def second_product(g):
             for n in range(SLICES):
                 if g == 0:
-                    y_acc.append(psum.tile([P, BANK], F32, name=f"y_acc{n}", tag="bank"))
+                    y_acc.append(bank(f"y_acc{n}", "h_bank" if n < 4 else "d_bank" if n < 6 else "r_bank"))
                 which = g * (H // BANK) + n // PACK
                 cols = slice((n % PACK) * P, (n % PACK + 1) * P)
                 nc.tensor.matmul_mx(
@@ -233,33 +258,38 @@ def tile_list_tilt_register_scores_kernel(
                     stop=(g == PASSES2 - 1),
                 )
 
+        pages.append(load_page(2))
+        olds = [fetch_old(0)]
         hs = [features(0)]
-        rises = [excess(0, hs[0], HALVES)]
+        rises = [excess(0, hs[0], olds[0])]
+        olds.append(fetch_old(1))
         hs.append(features(1))
-        rises.append(excess(1, hs[1], 1))
+        rises.append(excess(1, hs[1], olds[1]))
+        olds.append(fetch_old(2))
         soil_out = None
         for s in range(SLICES):
-            if s + 2 < SLICES:
-                pages.append(load_page(s + 2))
-                hs.append(features(s + 2))
+            if s + 3 < SLICES:
+                pages.append(load_page(s + 3))
             if s == 0:
                 load_soil_in(0)
+            if s == 2:
+                load_soil_in(1)
             if s == 3:
                 quantize_w2(0)
-            if s == 4:
-                load_soil_in(1)
             if s == 5:
                 quantize_w2(1)
             if s == 6:
                 soil_out = big_tile([P, SLICES, M], F32, "soil_out")
                 nc.sync.dma_start(out=soil_out[:], in_=soil.rearrange("(n p) m -> p n m", p=P))
-            nc.vector.tensor_tensor(pages[s][:].indirect(idx2[:]), hs[s][:], rises[s][:], ALU.add)
+            nc.vector.tensor_tensor(pages[s][:].indirect(idx2[:]), olds[s][:], rises[s][:], ALU.add)
+            if s + 3 < SLICES:
+                olds.append(fetch_old(s + 3))
             if s + 2 < SLICES:
-                rises.append(excess(s + 2, hs[s + 2], 1))
+                hs.append(features(s + 2))
+                rises.append(excess(s + 2, hs[s + 2], olds[s + 2]))
             if s == SLICES - 1:
-                read_page(s - 1, 1)
                 read_page(s, 2)
-            elif s < SLICES - 2:
+            else:
                 read_page(s, 1)
             if s == 3:
                 quantize_x(0, [nc.scalar.copy])
@@ -269,7 +299,11 @@ def tile_list_tilt_register_scores_kernel(
         second_product(1)
 
         for n in range(SLICES):
-            z = ring.tile([P, M], F32, name=f"z{n}", tag="z", bufs=4, align_bytes=64)
-            nc.vector.tensor_tensor(z[:], y_acc[n][:], soil_out[:, n, :], ALU.add)
-            nc.scalar.activation(z[:], z[:], ACT.Sigmoid)
-            nc.sync.dma_start(out=out[n * P : (n + 1) * P, :], in_=z[:])
+            pieces = 2 if n == SLICES - 1 else 1
+            width = M // pieces
+            for i in range(pieces):
+                cols = slice(i * width, (i + 1) * width)
+                z = soil_out[:, n, cols]
+                nc.vector.tensor_tensor(z, y_acc[n][:, cols], z, ALU.add)
+                nc.scalar.activation(z, z, ACT.Sigmoid)
+                nc.sync.dma_start(out=out[n * P : (n + 1) * P, cols], in_=z)

@@ -26,6 +26,18 @@ PASSES2 = H // K_PASS
 SLICES = H // P
 HALVES = S // BANK
 LIVE_ROWS = 100
+SLOT = 4 * T2
+TAB_AT = [0, 2 * SLOT, 0]
+ROCK_SCALE_AT = 4 * SLOT
+BIAS_AT = ROCK_SCALE_AT - 32
+ROCK_AT = 5 * SLOT
+SCALE_AT = 6 * SLOT
+SPARE_AT = 7 * SLOT
+W2_AT = 8 * SLOT
+SPARE2_AT = 10 * SLOT
+PAGE_AT = [ROCK_AT, 2 * SLOT, 0, SLOT, SPARE2_AT, SPARE_AT, ROCK_AT, 2 * SLOT]
+SOIL_AT = [3 * SLOT, 0]
+H_AT = [3 * SLOT, SPARE2_AT, SPARE_AT, W2_AT]
 
 
 def tile_list_tilt_register_scores_kernel(
@@ -36,17 +48,17 @@ def tile_list_tilt_register_scores_kernel(
         lists = ctx.enter_context(tc.tile_pool(name="lists", bufs=1))
         keep = ctx.enter_context(tc.tile_pool(name="keep", bufs=1))
         ring = ctx.enter_context(tc.tile_pool(name="ring", bufs=1))
+        arena = ctx.enter_context(tc.tile_pool(name="arena", bufs=1))
         psum = ctx.enter_context(tc.psum_pool(name="psum", bufs=1))
 
         idx = lists.tile([P, S // 16], U16, name="idx")
         idx2 = lists.tile([P, S // 16], U16, name="idx2")
         idx3 = lists.tile([P, M // 16], U16, name="idx3")
 
-        tab_scale_rows = keep.tile([P, T], U8, name="tab_scale_rows", tag="tab_scale_rows", align_bytes=64)
-        rock_scale_rows = keep.tile([P, PASSES1, H], U8, name="rock_scale_rows", tag="rock_scale_rows", align_bytes=64)
+        tab_scale_rows = arena.tile([P, T], U8, name="tab_scale_rows", offset=SCALE_AT, align_bytes=64)
+        rock_scale_rows = arena.tile([P, PASSES1, H], U8, name="rock_scale_rows", offset=ROCK_SCALE_AT, align_bytes=64)
         v_planes = [keep.tile([P, S], U8, name=f"v_plane{a}", align_bytes=64) for a in range(PASSES1)]
-        nc.gpsimd.memset(tab_scale_rows[:].bitcast(I32), 0)
-        nc.vector.memset(rock_scale_rows[:].bitcast(I32), 0)
+        nc.vector.memset(tab_scale_rows[:].bitcast(I32), 0)
         for a in range(1, PASSES1):
             nc.vector.memset(v_planes[a][:].bitcast(I32), 0)
         identity = keep.tile([P, P], F32, name="identity", align_bytes=64)
@@ -54,11 +66,11 @@ def tile_list_tilt_register_scores_kernel(
         def bank(name, tag):
             return psum.tile([P, BANK], F32, name=name, tag=tag, bufs=4 if tag == "h_bank" else 2)
 
-        def big_tile(shape, dtype, name):
-            return ring.tile(shape, dtype, name=name, tag="big", bufs=3, align_bytes=64)
+        def placed(shape, dtype, name, at):
+            return arena.tile(shape, dtype, name=name, offset=at, align_bytes=64)
 
         def load_table(a):
-            words = big_tile([P, T], U32, f"tab{a}")
+            words = placed([P, T], U32, f"tab{a}", TAB_AT[a])
             nc.sync.dma_start(
                 out=words[:].bitcast(I32), in_=tab_words[a].rearrange("p t i -> p (t i)").bitcast(I32)
             )
@@ -66,41 +78,40 @@ def tile_list_tilt_register_scores_kernel(
 
         def load_page(s):
             g, t = divmod(s, PACK)
-            page = ring.tile([P, T2], F32, name=f"page{s}", tag="page", bufs=6, align_bytes=64)
+            page = placed([P, T2], F32, f"page{s}", PAGE_AT[s])
             rows = page0[g * K_PASS : (g + 1) * K_PASS, :].rearrange("(p t) c -> t p c", t=PACK)
             nc.sync.dma_start(out=page[:], in_=rows[t])
             return page
 
+        bias = arena.tile([P, PASSES2, 2 * PACK], F32, name="bias", offset=BIAS_AT)
+        nc.sync.dma_start(out=bias[:, :, 0:PACK], in_=b1.rearrange("(g p t) -> p g t", p=P, t=PACK))
+        nc.sync.dma_start(idx[:], offs)
+        nc.sync.dma_start(idx2[:], offs2)
+        nc.sync.dma_start(idx3[:], offs3)
+        gain = keep.tile([P, PASSES2, PACK], F32, name="gain")
+        nc.sync.dma_start(out=gain[:], in_=gs.rearrange("(g p t) -> p g t", p=P, t=PACK))
+        neg_bias = keep.tile([P, PASSES2, PACK], F32, name="neg_bias")
+        nc.scalar.mul(neg_bias[:], bias[:, :, 0:PACK], -1.0)
+        nc.gpsimd.memset(rock_scale_rows[:].bitcast(I32), 0)
         tabs = [load_table(0)]
+        rock_raw = placed([P, PASSES1, 2 * H], U8, "rock_raw", ROCK_AT)
+        nc.sync.dma_start(out=rock_raw[:].bitcast(I32), in_=rock_words.rearrange("a p c -> p a c").bitcast(I32))
         for q in range(4):
-            nc.gpsimd.dma_start(
+            nc.sync.dma_start(
                 out=tab_scale_rows[32 * q : 32 * q + 4 * PASSES1, :].bitcast(I32),
                 in_=tab_scales[:, 4 * q : 4 * q + 4, :].bitcast(I32),
             )
-        nc.sync.dma_start(idx[:], offs)
-        rock_raw = keep.tile([P, PASSES1, 2 * H], U8, name="rock_raw", align_bytes=64)
-        nc.sync.dma_start(out=rock_raw[:].bitcast(I32), in_=rock_words.rearrange("a p c -> p a c").bitcast(I32))
         tabs.append(load_table(1))
         for q in range(4):
-            nc.gpsimd.dma_start(
+            nc.sync.dma_start(
                 out=rock_scale_rows[32 * q : 32 * q + 4, :, :].bitcast(I32),
                 in_=rock_scales[:, 4 * q : 4 * q + 4, :].rearrange("a r c -> r a c").bitcast(I32),
             )
         make_identity(nc, identity[:])
-        tabs.append(load_table(2))
-        bias = keep.tile([P, PASSES2, PACK], F32, name="bias")
-        nc.sync.dma_start(out=bias[:], in_=b1.rearrange("(g p t) -> p g t", p=P, t=PACK))
-        neg_bias = keep.tile([P, PASSES2, PACK], F32, name="neg_bias")
-        nc.scalar.mul(neg_bias[:], bias[:], -1.0)
-        nc.sync.dma_start(idx2[:], offs2)
-        pages = [load_page(0), load_page(1)]
-        nc.sync.dma_start(idx3[:], offs3)
-        gain = keep.tile([P, PASSES2, PACK], F32, name="gain")
-        nc.sync.dma_start(out=gain[:], in_=gs.rearrange("(g p t) -> p g t", p=P, t=PACK))
 
         nc.vector.tensor_copy(v_planes[0][:], tab_scale_rows[:].indirect(idx[:]))
         for a in range(1, PASSES1):
-            nc.gpsimd.dma_start(
+            nc.sync.dma_start(
                 out=v_planes[a][0:LIVE_ROWS, :].bitcast(I32),
                 in_=v_planes[0][4 * a : 4 * a + LIVE_ROWS, :].bitcast(I32),
             )
@@ -109,7 +120,10 @@ def tile_list_tilt_register_scores_kernel(
         rock_planes = []
         v_words = []
         for a in range(PASSES1):
-            codes = keep.tile([P, 2 * H], U8, name=f"rock_codes{a}", align_bytes=64)
+            if a == PASSES1 - 1:
+                codes = placed([P, 2 * H], U8, f"rock_codes{a}", SCALE_AT)
+            else:
+                codes = keep.tile([P, 2 * H], U8, name=f"rock_codes{a}", tag=f"rock_codes{a}", align_bytes=64)
             nc.vector.tensor_copy(
                 out=codes[:].bitcast(U16).rearrange("p (g t q) -> p g t q", g=PASSES2, t=PACK),
                 in_=rock_raw[:, a, :].bitcast(U16).rearrange("p (g q t) -> p g t q", g=PASSES2, t=PACK),
@@ -123,19 +137,19 @@ def tile_list_tilt_register_scores_kernel(
             rock_planes.append(plane)
             picked = []
             for half in range(HALVES):
-                tag = "tab_scale_rows" if (a, half) == (0, 1) else "rock_scale_rows" if (a, half) == (2, 0) else f"v_words{a}_{half}"
-                words = keep.tile([P, BANK], U32, name=f"v_words{a}_{half}", tag=tag, align_bytes=64)
+                words = keep.tile([P, BANK], U32, name=f"v_words{a}_{half}", tag=f"v_words{a}_{half}", align_bytes=64)
                 cols = slice(half * BANK // 16, (half + 1) * BANK // 16)
                 nc.vector.tensor_copy(words[:], tabs[a][:].indirect(idx[:, cols]))
                 picked.append(words)
             v_words.append(picked)
+            if a == 0:
+                tabs.append(load_table(2))
 
+        pages = [load_page(s) for s in range(3)]
         soil_in = []
-        for g in range(PASSES2):
-            tile = keep.tile([P, PACK, M], F32, name=f"soil_in{g}", align_bytes=64)
-            soil_in.append(tile)
 
         def load_soil_in(g):
+            soil_in.append(placed([P, PACK, M], F32, f"soil_in{g}", SOIL_AT[g]))
             nc.sync.dma_start(
                 out=soil_in[g][:], in_=soil[g * K_PASS : (g + 1) * K_PASS, :].rearrange("(p t) m -> p t m", t=PACK)
             )
@@ -144,7 +158,10 @@ def tile_list_tilt_register_scores_kernel(
 
         def features(s):
             g, t = divmod(s, PACK)
-            h = ring.tile([P, S], F32, name=f"h{s}", tag="h", bufs=4, align_bytes=64)
+            if s < len(H_AT):
+                h = placed([P, S], F32, f"h{s}", H_AT[s])
+            else:
+                h = ring.tile([P, S], F32, name=f"h{s}", tag="h", bufs=4, align_bytes=64)
             for half in range(HALVES):
                 cols = slice(half * BANK, (half + 1) * BANK)
                 acc = bank(f"h_acc{s}_{half}", "h_bank")
@@ -163,7 +180,11 @@ def tile_list_tilt_register_scores_kernel(
 
         def fetch_old(s):
             old = ring.tile([P, S], F32, name=f"old{s}", tag="old", bufs=4, align_bytes=64)
-            nc.vector.tensor_copy(old[:], pages[s][:].indirect(idx2[:]))
+            pieces = HALVES if s == 0 else 1
+            width = S // pieces
+            for i in range(pieces):
+                entries = idx2[:, i * width // 16 : (i + 1) * width // 16]
+                nc.vector.tensor_copy(old[:, i * width : (i + 1) * width], pages[s][:].indirect(entries))
             return old
 
         def excess(s, neg_h, old):
@@ -196,21 +217,29 @@ def tile_list_tilt_register_scores_kernel(
         w_codes = []
         w_planes = []
 
-        def quantize_w2(g):
-            raw = big_tile([P, PACK, H], F32, f"w2_raw{g}")
+        w_woven = []
+
+        def weave_w2(g):
+            raw = placed([P, PACK, H], F32, f"w2_raw{g}", W2_AT)
             nc.sync.dma_start(
                 out=raw[:], in_=w2[g * K_PASS : (g + 1) * K_PASS, :].rearrange("(p t) n -> p t n", t=PACK)
             )
             for half in range(H // BANK):
-                woven = ring.tile([P, BANK, PACK], BF16, name=f"w2_woven{g}_{half}", tag="woven", bufs=2, align_bytes=64)
+                woven = ring.tile([P, BANK, PACK], BF16, name=f"w2_woven{g}_{half}", tag="woven", bufs=3, align_bytes=64)
                 interleave(nc.scalar.copy, woven[:], raw[:, :, half * BANK : (half + 1) * BANK])
+                w_woven.append(woven)
+
+        def quantize_w2(g, half):
+            if g == 0:
                 codes = keep.tile([P, BANK], U32, name=f"w_codes{g}_{half}", align_bytes=64)
-                plane = keep.tile([P, BANK], U8, name=f"w_plane{g}_{half}", align_bytes=64)
-                nc.vector.quantize_mx(
-                    out=codes[:].bitcast(FP8X4), scales=plane[:], in_=woven[:].rearrange("p c t -> p (c t)")
-                )
-                w_codes.append(codes)
-                w_planes.append(plane)
+            else:
+                codes = placed([P, BANK], U32, f"w_codes{g}_{half}", SOIL_AT[1] + half * 4 * BANK)
+            plane = keep.tile([P, BANK], U8, name=f"w_plane{g}_{half}", align_bytes=64)
+            nc.vector.quantize_mx(
+                out=codes[:].bitcast(FP8X4), scales=plane[:], in_=w_woven[2 * g + half][:].rearrange("p c t -> p (c t)")
+            )
+            w_codes.append(codes)
+            w_planes.append(plane)
 
         x_rows = []
 
@@ -229,7 +258,7 @@ def tile_list_tilt_register_scores_kernel(
         x_planes = []
 
         def quantize_x(g, copies):
-            woven = ring.tile([P, M, PACK], BF16, name=f"x_woven{g}", tag="woven", bufs=2, align_bytes=64)
+            woven = ring.tile([P, M, PACK], BF16, name=f"x_woven{g}", tag="woven", bufs=3, align_bytes=64)
             width = M // len(copies)
             for i, engine_copy in enumerate(copies):
                 cols = slice(i * width, (i + 1) * width)
@@ -258,7 +287,6 @@ def tile_list_tilt_register_scores_kernel(
                     stop=(g == PASSES2 - 1),
                 )
 
-        pages.append(load_page(2))
         olds = [fetch_old(0)]
         hs = [features(0)]
         rises = [excess(0, hs[0], olds[0])]
@@ -266,21 +294,23 @@ def tile_list_tilt_register_scores_kernel(
         hs.append(features(1))
         rises.append(excess(1, hs[1], olds[1]))
         olds.append(fetch_old(2))
-        soil_out = None
+        soil_out = []
         for s in range(SLICES):
             if s + 3 < SLICES:
                 pages.append(load_page(s + 3))
             if s == 0:
                 load_soil_in(0)
-            if s == 2:
-                load_soil_in(1)
             if s == 3:
-                quantize_w2(0)
+                weave_w2(0)
+                quantize_w2(0, 0)
+                quantize_w2(0, 1)
             if s == 5:
-                quantize_w2(1)
+                weave_w2(1)
             if s == 6:
-                soil_out = big_tile([P, SLICES, M], F32, "soil_out")
-                nc.sync.dma_start(out=soil_out[:], in_=soil.rearrange("(n p) m -> p n m", p=P))
+                spent = ["v_words0_1", "v_words2_0", "v_words0_0", "v_words1_0", "v_words1_1", "v_words2_1", "rock_codes0", "rock_codes1"]
+                for n in range(SLICES):
+                    soil_out.append(keep.tile([P, M], F32, name=f"soil_out{n}", tag=spent[n], align_bytes=64))
+                    nc.sync.dma_start(out=soil_out[n][:], in_=soil[n * P : (n + 1) * P, :])
             nc.vector.tensor_tensor(pages[s][:].indirect(idx2[:]), olds[s][:], rises[s][:], ALU.add)
             if s + 3 < SLICES:
                 olds.append(fetch_old(s + 3))
@@ -291,11 +321,15 @@ def tile_list_tilt_register_scores_kernel(
                 read_page(s, 2)
             else:
                 read_page(s, 1)
+            if s == 2:
+                load_soil_in(1)
             if s == 3:
                 quantize_x(0, [nc.scalar.copy])
             if s == 5:
                 second_product(0)
+        quantize_w2(1, 0)
         quantize_x(1, [nc.scalar.copy, nc.vector.tensor_copy])
+        quantize_w2(1, 1)
         second_product(1)
 
         for n in range(SLICES):
@@ -303,7 +337,7 @@ def tile_list_tilt_register_scores_kernel(
             width = M // pieces
             for i in range(pieces):
                 cols = slice(i * width, (i + 1) * width)
-                z = soil_out[:, n, cols]
+                z = soil_out[n][:, cols]
                 nc.vector.tensor_tensor(z, y_acc[n][:, cols], z, ALU.add)
                 nc.scalar.activation(z, z, ACT.Sigmoid)
                 nc.sync.dma_start(out=out[n * P : (n + 1) * P, cols], in_=z)

@@ -21,23 +21,26 @@ P = 128
 PACK = 4
 K_PASS = P * PACK
 BANK = 512
+QUADRANTS = 4
 PASSES1 = K // K_PASS
 PASSES2 = H // K_PASS
 SLICES = H // P
 HALVES = S // BANK
-LIVE_ROWS = 100
-SLOT = 4 * T2
-TAB_AT = [0, 2 * SLOT, 0]
-ROCK_SCALE_AT = 4 * SLOT
-BIAS_AT = ROCK_SCALE_AT - 32
-ROCK_AT = 5 * SLOT
-SCALE_AT = 6 * SLOT
-SPARE_AT = 7 * SLOT
-W2_AT = 8 * SLOT
-SPARE2_AT = 10 * SLOT
-PAGE_AT = [ROCK_AT, 2 * SLOT, 0, SLOT, SPARE2_AT, SPARE_AT, ROCK_AT, 2 * SLOT]
-SOIL_AT = [3 * SLOT, 0]
-H_AT = [3 * SLOT, SPARE2_AT, SPARE_AT, W2_AT]
+LINE = 16
+PLANE_ROWS = 32 * (QUADRANTS - 1) + 4
+
+KB = 1024
+TAB_AT = [15 * KB, 32 * KB, 0]
+PICKED_SCALES_AT = 30 * KB
+ROCK_SCALES_AT = 48 * KB
+BIAS_AT = ROCK_SCALES_AT - 32
+ROCK_AT = 52 * KB
+TAB_SCALES_AT = 60 * KB
+W2_AT = 72 * KB
+PAGE_AT = [ROCK_AT, TAB_AT[1], TAB_AT[2], TAB_AT[2] + 8 * KB, 64 * KB, 16 * KB, ROCK_AT, TAB_AT[1]]
+SOIL_AT = [TAB_AT[1] + 8 * KB, PAGE_AT[2]]
+FEATURES_AT = [SOIL_AT[0], PAGE_AT[4], PAGE_AT[5], W2_AT]
+TURNED_AT = [88 * KB, 92 * KB, 96 * KB]
 
 
 def tile_list_tilt_register_scores_kernel(
@@ -51,23 +54,27 @@ def tile_list_tilt_register_scores_kernel(
         arena = ctx.enter_context(tc.tile_pool(name="arena", bufs=1))
         psum = ctx.enter_context(tc.psum_pool(name="psum", bufs=1))
 
-        idx = lists.tile([P, S // 16], U16, name="idx")
-        idx2 = lists.tile([P, S // 16], U16, name="idx2")
-        idx3 = lists.tile([P, M // 16], U16, name="idx3")
-
-        tab_scale_rows = arena.tile([P, T], U8, name="tab_scale_rows", offset=SCALE_AT, align_bytes=64)
-        rock_scale_rows = arena.tile([P, PASSES1, H], U8, name="rock_scale_rows", offset=ROCK_SCALE_AT, align_bytes=64)
-        v_planes = [keep.tile([P, S], U8, name=f"v_plane{a}", align_bytes=64) for a in range(PASSES1)]
-        nc.vector.memset(tab_scale_rows[:].bitcast(I32), 0)
-        for a in range(1, PASSES1):
-            nc.vector.memset(v_planes[a][:].bitcast(I32), 0)
-        identity = keep.tile([P, P], F32, name="identity", align_bytes=64)
+        def placed(shape, dtype, name, at):
+            return arena.tile(shape, dtype, name=name, offset=at, align_bytes=64)
 
         def bank(name, tag):
             return psum.tile([P, BANK], F32, name=name, tag=tag, bufs=4 if tag == "h_bank" else 2)
 
-        def placed(shape, dtype, name, at):
-            return arena.tile(shape, dtype, name=name, offset=at, align_bytes=64)
+        def entries(offsets, first, count):
+            return offsets[:, first // 16 : (first + count) // 16]
+
+        idx = lists.tile([P, S // 16], U16, name="idx")
+        idx2 = lists.tile([P, S // 16], U16, name="idx2")
+        idx3 = lists.tile([P, M // 16], U16, name="idx3")
+
+        tab_scale_rows = placed([P, T], U8, "tab_scale_rows", TAB_SCALES_AT)
+        rock_scale_rows = placed([P, PASSES1, H], U8, "rock_scale_rows", ROCK_SCALES_AT)
+        v_planes = [placed([P, S], U8, "v_plane0", PICKED_SCALES_AT)]
+        v_planes.extend(keep.tile([P, S], U8, name=f"v_plane{a}", align_bytes=64) for a in range(1, PASSES1))
+        nc.vector.memset(tab_scale_rows[:].bitcast(I32), 0)
+        for a in range(1, PASSES1):
+            nc.vector.memset(v_planes[a][:].bitcast(I32), 0)
+        identity = keep.tile([P, P], F32, name="identity", align_bytes=64)
 
         def load_table(a):
             words = placed([P, T], U32, f"tab{a}", TAB_AT[a])
@@ -84,66 +91,70 @@ def tile_list_tilt_register_scores_kernel(
             return page
 
         bias = arena.tile([P, PASSES2, 2 * PACK], F32, name="bias", offset=BIAS_AT)
-        nc.sync.dma_start(out=bias[:, :, 0:PACK], in_=b1.rearrange("(g p t) -> p g t", p=P, t=PACK))
+        nc.scalar.dma_start(out=bias[:, :, 0:PACK], in_=b1.rearrange("(g p t) -> p g t", p=P, t=PACK))
         nc.sync.dma_start(idx[:], offs)
         nc.sync.dma_start(idx2[:], offs2)
         nc.sync.dma_start(idx3[:], offs3)
         gain = keep.tile([P, PASSES2, PACK], F32, name="gain")
-        nc.sync.dma_start(out=gain[:], in_=gs.rearrange("(g p t) -> p g t", p=P, t=PACK))
+        nc.scalar.dma_start(out=gain[:], in_=gs.rearrange("(g p t) -> p g t", p=P, t=PACK))
         neg_bias = keep.tile([P, PASSES2, PACK], F32, name="neg_bias")
         nc.scalar.mul(neg_bias[:], bias[:, :, 0:PACK], -1.0)
         nc.gpsimd.memset(rock_scale_rows[:].bitcast(I32), 0)
+
         tabs = [load_table(0)]
         rock_raw = placed([P, PASSES1, 2 * H], U8, "rock_raw", ROCK_AT)
         nc.sync.dma_start(out=rock_raw[:].bitcast(I32), in_=rock_words.rearrange("a p c -> p a c").bitcast(I32))
-        for q in range(4):
+        for q in range(QUADRANTS):
             nc.sync.dma_start(
                 out=tab_scale_rows[32 * q : 32 * q + 4 * PASSES1, :].bitcast(I32),
                 in_=tab_scales[:, 4 * q : 4 * q + 4, :].bitcast(I32),
             )
         tabs.append(load_table(1))
-        for q in range(4):
+        for q in range(QUADRANTS):
             nc.sync.dma_start(
                 out=rock_scale_rows[32 * q : 32 * q + 4, :, :].bitcast(I32),
                 in_=rock_scales[:, 4 * q : 4 * q + 4, :].rearrange("a r c -> r a c").bitcast(I32),
             )
         make_identity(nc, identity[:])
 
+        def pick_words(a):
+            picked = []
+            for half in range(HALVES):
+                name = f"v_words{a}_{half}"
+                words = keep.tile([P, BANK], U32, name=name, tag=name, align_bytes=64)
+                nc.vector.tensor_copy(words[:], tabs[a][:].indirect(entries(idx, half * BANK, BANK)))
+                picked.append(words)
+            return picked
+
+        v_words = [pick_words(0)]
+        tabs.append(load_table(2))
         nc.vector.tensor_copy(v_planes[0][:], tab_scale_rows[:].indirect(idx[:]))
         for a in range(1, PASSES1):
             nc.sync.dma_start(
-                out=v_planes[a][0:LIVE_ROWS, :].bitcast(I32),
-                in_=v_planes[0][4 * a : 4 * a + LIVE_ROWS, :].bitcast(I32),
+                out=v_planes[a][0:PLANE_ROWS, :].bitcast(I32),
+                in_=v_planes[0][4 * a : 4 * a + PLANE_ROWS, :].bitcast(I32),
             )
 
         rock_codes = []
         rock_planes = []
-        v_words = []
         for a in range(PASSES1):
-            if a == PASSES1 - 1:
-                codes = placed([P, 2 * H], U8, f"rock_codes{a}", SCALE_AT)
+            name = f"rock_codes{a}"
+            if a == 0:
+                codes = placed([P, 2 * H], U8, name, TAB_SCALES_AT)
             else:
-                codes = keep.tile([P, 2 * H], U8, name=f"rock_codes{a}", tag=f"rock_codes{a}", align_bytes=64)
+                codes = keep.tile([P, 2 * H], U8, name=name, tag=name, align_bytes=64)
             nc.vector.tensor_copy(
-                out=codes[:].bitcast(U16).rearrange("p (g t q) -> p g t q", g=PASSES2, t=PACK),
-                in_=rock_raw[:, a, :].bitcast(U16).rearrange("p (g q t) -> p g t q", g=PASSES2, t=PACK),
+                out=codes[:].bitcast(U16).rearrange("p (g t c q) -> p g c t q", g=PASSES2, t=PACK, q=LINE // 2),
+                in_=rock_raw[:, a, :].bitcast(U16).rearrange("p (g c q t) -> p g c t q", g=PASSES2, t=PACK, q=LINE // 2),
             )
             rock_codes.append(codes)
             plane = keep.tile([P, H], U8, name=f"rock_plane{a}", align_bytes=64)
             nc.vector.tensor_copy(
-                out=plane[:].rearrange("p (g t q) -> p g t q", g=PASSES2, t=PACK),
-                in_=rock_scale_rows[:, a, :].rearrange("p (g q t) -> p g t q", g=PASSES2, t=PACK),
+                out=plane[:].rearrange("p (g t c q) -> p g c t q", g=PASSES2, t=PACK, q=LINE),
+                in_=rock_scale_rows[:, a, :].rearrange("p (g c q t) -> p g c t q", g=PASSES2, t=PACK, q=LINE),
             )
             rock_planes.append(plane)
-            picked = []
-            for half in range(HALVES):
-                words = keep.tile([P, BANK], U32, name=f"v_words{a}_{half}", tag=f"v_words{a}_{half}", align_bytes=64)
-                cols = slice(half * BANK // 16, (half + 1) * BANK // 16)
-                nc.vector.tensor_copy(words[:], tabs[a][:].indirect(idx[:, cols]))
-                picked.append(words)
-            v_words.append(picked)
-            if a == 0:
-                tabs.append(load_table(2))
+        v_words.extend(pick_words(a) for a in range(1, PASSES1))
 
         pages = [load_page(s) for s in range(3)]
         soil_in = []
@@ -153,15 +164,13 @@ def tile_list_tilt_register_scores_kernel(
             nc.sync.dma_start(
                 out=soil_in[g][:], in_=soil[g * K_PASS : (g + 1) * K_PASS, :].rearrange("(p t) m -> p t m", t=PACK)
             )
-            for t in range(PACK):
-                nc.scalar.activation(soil_in[g][:, t, :], soil_in[g][:, t, :], ACT.Copy, scale=gain[:, g, t : t + 1])
 
-        def features(s):
+        def negated_features(s):
             g, t = divmod(s, PACK)
-            if s < len(H_AT):
-                h = placed([P, S], F32, f"h{s}", H_AT[s])
+            if s < len(FEATURES_AT):
+                neg_h = placed([P, S], F32, f"neg_h{s}", FEATURES_AT[s])
             else:
-                h = ring.tile([P, S], F32, name=f"h{s}", tag="h", bufs=4, align_bytes=64)
+                neg_h = ring.tile([P, S], F32, name=f"neg_h{s}", tag="neg_h", bufs=SLICES - len(FEATURES_AT), align_bytes=64)
             for half in range(HALVES):
                 cols = slice(half * BANK, (half + 1) * BANK)
                 acc = bank(f"h_acc{s}_{half}", "h_bank")
@@ -175,20 +184,20 @@ def tile_list_tilt_register_scores_kernel(
                         start=(a == 0),
                         stop=(a == PASSES1 - 1),
                     )
-                nc.scalar.activation(h[:, cols], acc[:], ACT.Identity, bias=neg_bias[:, g, t : t + 1], scale=-1.0)
-            return h
+                nc.scalar.activation(neg_h[:, cols], acc[:], ACT.Identity, bias=neg_bias[:, g, t : t + 1], scale=-1.0)
+            return neg_h
 
         def fetch_old(s):
-            old = ring.tile([P, S], F32, name=f"old{s}", tag="old", bufs=4, align_bytes=64)
+            old = ring.tile([P, S], F32, name=f"old{s}", tag="old", bufs=SLICES, align_bytes=64)
             pieces = HALVES if s == 0 else 1
             width = S // pieces
             for i in range(pieces):
-                entries = idx2[:, i * width // 16 : (i + 1) * width // 16]
-                nc.vector.tensor_copy(old[:, i * width : (i + 1) * width], pages[s][:].indirect(entries))
+                window = pages[s][:].indirect(entries(idx2, i * width, width))
+                nc.vector.tensor_copy(old[:, i * width : (i + 1) * width], window)
             return old
 
-        def excess(s, neg_h, old):
-            turned = ring.tile([P, S], F32, name=f"turned{s}", tag="turned", bufs=2, align_bytes=64)
+        def rise_over(s, neg_h, old):
+            turned = placed([P, S], F32, f"turned{s}", TURNED_AT[s % len(TURNED_AT)])
             rise = ring.tile([P, S], F32, name=f"rise{s}", tag="rise", bufs=2, align_bytes=64)
             for half in range(HALVES):
                 cols = slice(half * BANK, (half + 1) * BANK)
@@ -208,15 +217,17 @@ def tile_list_tilt_register_scores_kernel(
                 nc.scalar.copy(rise[:, cols], back[:])
             return rise
 
-        def interleave(engine_copy, dst, src):
+        def weave(engine_copy, dst, src):
             engine_copy(
-                out=dst.rearrange("p (c i) t -> p c t i", i=4),
-                in_=src.rearrange("p t (c i) -> p c t i", i=4),
+                out=dst.rearrange("p (c i) t -> p c t i", i=LINE // 4),
+                in_=src.rearrange("p t (c i) -> p c t i", i=LINE // 4),
             )
+
+        def woven_tile(name):
+            return ring.tile([P, BANK, PACK], BF16, name=name, tag="woven", bufs=3, align_bytes=64)
 
         w_codes = []
         w_planes = []
-
         w_woven = []
 
         def weave_w2(g):
@@ -225,18 +236,20 @@ def tile_list_tilt_register_scores_kernel(
                 out=raw[:], in_=w2[g * K_PASS : (g + 1) * K_PASS, :].rearrange("(p t) n -> p t n", t=PACK)
             )
             for half in range(H // BANK):
-                woven = ring.tile([P, BANK, PACK], BF16, name=f"w2_woven{g}_{half}", tag="woven", bufs=3, align_bytes=64)
-                interleave(nc.scalar.copy, woven[:], raw[:, :, half * BANK : (half + 1) * BANK])
+                woven = woven_tile(f"w2_woven{g}_{half}")
+                weave(nc.scalar.copy, woven[:], raw[:, :, half * BANK : (half + 1) * BANK])
                 w_woven.append(woven)
 
         def quantize_w2(g, half):
+            name = f"w_codes{g}_{half}"
             if g == 0:
-                codes = keep.tile([P, BANK], U32, name=f"w_codes{g}_{half}", align_bytes=64)
+                codes = keep.tile([P, BANK], U32, name=name, align_bytes=64)
             else:
-                codes = placed([P, BANK], U32, f"w_codes{g}_{half}", SOIL_AT[1] + half * 4 * BANK)
+                codes = placed([P, BANK], U32, name, TURNED_AT[SLICES % len(TURNED_AT)] + half * 2 * KB)
             plane = keep.tile([P, BANK], U8, name=f"w_plane{g}_{half}", align_bytes=64)
+            woven = w_woven[g * (H // BANK) + half]
             nc.vector.quantize_mx(
-                out=codes[:].bitcast(FP8X4), scales=plane[:], in_=w_woven[2 * g + half][:].rearrange("p c t -> p (c t)")
+                out=codes[:].bitcast(FP8X4), scales=plane[:], in_=woven[:].rearrange("p c t -> p (c t)")
             )
             w_codes.append(codes)
             w_planes.append(plane)
@@ -247,22 +260,24 @@ def tile_list_tilt_register_scores_kernel(
             g, t = divmod(s, PACK)
             if t == 0:
                 x_rows.append(ring.tile([P, PACK, M], F32, name=f"x_rows{g}", tag="x_rows", bufs=1, align_bytes=64))
+            scaled = placed([P, M], F32, f"scaled_soil{s}", TURNED_AT[(s + 1) % len(TURNED_AT)] + KB)
+            nc.scalar.activation(scaled[:], soil_in[g][:, t, :], ACT.Copy, scale=gain[:, g, t : t + 1])
             width = M // pieces
             for i in range(pieces):
                 cols = slice(i * width, (i + 1) * width)
-                entries = idx3[:, i * width // 16 : (i + 1) * width // 16]
-                nc.vector.tensor_tensor(x_rows[g][:, t, cols], pages[s][:].indirect(entries), soil_in[g][:, t, cols], ALU.add)
+                window = pages[s][:].indirect(entries(idx3, i * width, width))
+                nc.vector.tensor_tensor(x_rows[g][:, t, cols], window, scaled[:, cols], ALU.add)
 
         y_acc = []
         x_codes = []
         x_planes = []
 
         def quantize_x(g, copies):
-            woven = ring.tile([P, M, PACK], BF16, name=f"x_woven{g}", tag="woven", bufs=3, align_bytes=64)
+            woven = woven_tile(f"x_woven{g}")
             width = M // len(copies)
             for i, engine_copy in enumerate(copies):
                 cols = slice(i * width, (i + 1) * width)
-                interleave(engine_copy, woven[:, cols, :], x_rows[g][:, :, cols])
+                weave(engine_copy, woven[:, cols, :], x_rows[g][:, :, cols])
             codes = keep.tile([P, M], U32, name=f"x_codes{g}", align_bytes=64)
             plane = keep.tile([P, M], U8, name=f"x_plane{g}", align_bytes=64)
             nc.vector.quantize_mx(
@@ -271,12 +286,15 @@ def tile_list_tilt_register_scores_kernel(
             x_codes.append(codes)
             x_planes.append(plane)
 
+        y_tags = 4 * ["h_bank"] + 2 * ["d_bank"] + 2 * ["r_bank"]
+
         def second_product(g):
+            tiles_in_half = BANK // P
             for n in range(SLICES):
                 if g == 0:
-                    y_acc.append(bank(f"y_acc{n}", "h_bank" if n < 4 else "d_bank" if n < 6 else "r_bank"))
-                which = g * (H // BANK) + n // PACK
-                cols = slice((n % PACK) * P, (n % PACK + 1) * P)
+                    y_acc.append(bank(f"y_acc{n}", y_tags[n]))
+                which = g * (H // BANK) + n // tiles_in_half
+                cols = slice((n % tiles_in_half) * P, (n % tiles_in_half + 1) * P)
                 nc.tensor.matmul_mx(
                     out=y_acc[n][:],
                     lhsT=w_codes[which][:, cols].bitcast(FP8X4),
@@ -288,45 +306,40 @@ def tile_list_tilt_register_scores_kernel(
                 )
 
         olds = [fetch_old(0)]
-        hs = [features(0)]
-        rises = [excess(0, hs[0], olds[0])]
+        rises = [rise_over(0, negated_features(0), olds[0])]
         olds.append(fetch_old(1))
-        hs.append(features(1))
-        rises.append(excess(1, hs[1], olds[1]))
+        rises.append(rise_over(1, negated_features(1), olds[1]))
         olds.append(fetch_old(2))
+        pages.append(load_page(3))
+        olds.append(fetch_old(3))
+        load_soil_in(0)
         soil_out = []
         for s in range(SLICES):
-            if s + 3 < SLICES:
-                pages.append(load_page(s + 3))
-            if s == 0:
-                load_soil_in(0)
-            if s == 3:
+            nc.vector.tensor_tensor(pages[s][:].indirect(idx2[:]), olds[s][:], rises[s][:], ALU.add)
+            if s > 0:
+                read_page(s - 1, 1)
+            if s + 2 < SLICES:
+                rises.append(rise_over(s + 2, negated_features(s + 2), olds[s + 2]))
+            if s + 4 < SLICES:
+                pages.append(load_page(s + 4))
+                olds.append(fetch_old(s + 4))
+            if s + 2 == len(FEATURES_AT) - 1:
                 weave_w2(0)
                 quantize_w2(0, 0)
                 quantize_w2(0, 1)
-            if s == 5:
+            if s - 1 == 2:
+                load_soil_in(1)
+            if s - 1 == PACK - 1:
+                quantize_x(0, [nc.scalar.copy])
                 weave_w2(1)
-            if s == 6:
-                spent = ["v_words0_1", "v_words2_0", "v_words0_0", "v_words1_0", "v_words1_1", "v_words2_1", "rock_codes0", "rock_codes1"]
+            if s + 2 == SLICES - 1:
+                second_product(0)
+                spent = ["v_words0_1", "v_words2_0", "v_words0_0", "v_words1_0", "v_words1_1", "v_words2_1"]
+                spent.extend(["rock_codes2", "rock_codes1"])
                 for n in range(SLICES):
                     soil_out.append(keep.tile([P, M], F32, name=f"soil_out{n}", tag=spent[n], align_bytes=64))
                     nc.sync.dma_start(out=soil_out[n][:], in_=soil[n * P : (n + 1) * P, :])
-            nc.vector.tensor_tensor(pages[s][:].indirect(idx2[:]), olds[s][:], rises[s][:], ALU.add)
-            if s + 3 < SLICES:
-                olds.append(fetch_old(s + 3))
-            if s + 2 < SLICES:
-                hs.append(features(s + 2))
-                rises.append(excess(s + 2, hs[s + 2], olds[s + 2]))
-            if s == SLICES - 1:
-                read_page(s, 2)
-            else:
-                read_page(s, 1)
-            if s == 2:
-                load_soil_in(1)
-            if s == 3:
-                quantize_x(0, [nc.scalar.copy])
-            if s == 5:
-                second_product(0)
+        read_page(SLICES - 1, 2)
         quantize_w2(1, 0)
         quantize_x(1, [nc.scalar.copy, nc.vector.tensor_copy])
         quantize_w2(1, 1)

@@ -1,7 +1,6 @@
 from contextlib import ExitStack
 
 import concourse.mybir as mybir
-from concourse.masks import make_identity
 
 K, H, T, S, T2, M = 1536, 1024, 4096, 1024, 2048, 512
 FLOPS = 2 * K * H * S + 2 * H * H * M
@@ -27,6 +26,7 @@ PASSES2 = H // K_PASS
 SLICES = H // P
 HALVES = S // BANK
 LINE = 16
+LINK = 64
 PLANE_ROWS = 32 * (QUADRANTS - 1) + 4
 
 KB = 1024
@@ -34,13 +34,12 @@ TAB_AT = [15 * KB, 32 * KB, 0]
 PICKED_SCALES_AT = 30 * KB
 ROCK_SCALES_AT = 48 * KB
 BIAS_AT = ROCK_SCALES_AT - 32
-ROCK_AT = 52 * KB
-TAB_SCALES_AT = 60 * KB
-W2_AT = 72 * KB
-PAGE_AT = [ROCK_AT, TAB_AT[1], TAB_AT[2], TAB_AT[2] + 8 * KB, 64 * KB, 16 * KB, ROCK_AT, TAB_AT[1]]
-SOIL_AT = [TAB_AT[1] + 8 * KB, PAGE_AT[2]]
-FEATURES_AT = [SOIL_AT[0], PAGE_AT[4], PAGE_AT[5], W2_AT]
-TURNED_AT = [88 * KB, 92 * KB, 96 * KB]
+ROCK_AT = 56 * KB
+TAB_SCALES_AT = 64 * KB
+W2_AT = [68 * KB, 84 * KB]
+PAGE_AT = [ROCK_AT, TAB_AT[1], TAB_AT[1] + 8 * KB, ROCK_SCALES_AT, TAB_AT[2], 16 * KB, ROCK_AT, TAB_AT[1]]
+SOIL_AT = [TAB_AT[2] + 8 * KB, PAGE_AT[2]]
+FEATURES_AT = [PAGE_AT[5], W2_AT[0], W2_AT[1]]
 
 
 def tile_list_tilt_register_scores_kernel(
@@ -58,7 +57,7 @@ def tile_list_tilt_register_scores_kernel(
             return arena.tile(shape, dtype, name=name, offset=at, align_bytes=64)
 
         def bank(name, tag):
-            return psum.tile([P, BANK], F32, name=name, tag=tag, bufs=4 if tag == "h_bank" else 2)
+            return psum.tile([P, BANK], F32, name=name, tag=tag, bufs=HALVES if tag == "h_bank" else SLICES - HALVES)
 
         def entries(offsets, first, count):
             return offsets[:, first // 16 : (first + count) // 16]
@@ -74,7 +73,6 @@ def tile_list_tilt_register_scores_kernel(
         nc.vector.memset(tab_scale_rows[:].bitcast(I32), 0)
         for a in range(1, PASSES1):
             nc.vector.memset(v_planes[a][:].bitcast(I32), 0)
-        identity = keep.tile([P, P], F32, name="identity", align_bytes=64)
 
         def load_table(a):
             words = placed([P, T], U32, f"tab{a}", TAB_AT[a])
@@ -90,15 +88,15 @@ def tile_list_tilt_register_scores_kernel(
             nc.sync.dma_start(out=page[:], in_=rows[t])
             return page
 
-        bias = arena.tile([P, PASSES2, 2 * PACK], F32, name="bias", offset=BIAS_AT)
-        nc.scalar.dma_start(out=bias[:, :, 0:PACK], in_=b1.rearrange("(g p t) -> p g t", p=P, t=PACK))
+        bias_landing = arena.tile([P, PASSES2, 2 * PACK], F32, name="bias_landing", offset=BIAS_AT)
+        nc.scalar.dma_start(out=bias_landing[:, :, 0:PACK], in_=b1.rearrange("(g p t) -> p g t", p=P, t=PACK))
         nc.sync.dma_start(idx[:], offs)
         nc.sync.dma_start(idx2[:], offs2)
         nc.sync.dma_start(idx3[:], offs3)
         gain = keep.tile([P, PASSES2, PACK], F32, name="gain")
         nc.scalar.dma_start(out=gain[:], in_=gs.rearrange("(g p t) -> p g t", p=P, t=PACK))
-        neg_bias = keep.tile([P, PASSES2, PACK], F32, name="neg_bias")
-        nc.scalar.mul(neg_bias[:], bias[:, :, 0:PACK], -1.0)
+        bias = keep.tile([P, PASSES2, PACK], F32, name="bias")
+        nc.scalar.copy(bias[:], bias_landing[:, :, 0:PACK])
         nc.gpsimd.memset(rock_scale_rows[:].bitcast(I32), 0)
 
         tabs = [load_table(0)]
@@ -115,7 +113,6 @@ def tile_list_tilt_register_scores_kernel(
                 out=rock_scale_rows[32 * q : 32 * q + 4, :, :].bitcast(I32),
                 in_=rock_scales[:, 4 * q : 4 * q + 4, :].rearrange("a r c -> r a c").bitcast(I32),
             )
-        make_identity(nc, identity[:])
 
         def pick_words(a):
             picked = []
@@ -156,7 +153,7 @@ def tile_list_tilt_register_scores_kernel(
             rock_planes.append(plane)
         v_words.extend(pick_words(a) for a in range(1, PASSES1))
 
-        pages = [load_page(s) for s in range(3)]
+        pages = [load_page(s) for s in range(5)]
         soil_in = []
 
         def load_soil_in(g):
@@ -164,13 +161,16 @@ def tile_list_tilt_register_scores_kernel(
             nc.sync.dma_start(
                 out=soil_in[g][:], in_=soil[g * K_PASS : (g + 1) * K_PASS, :].rearrange("(p t) m -> p t m", t=PACK)
             )
+            for t in range(PACK):
+                rows = soil_in[g][:, t, :]
+                nc.scalar.activation(rows, rows, ACT.Copy, scale=gain[:, g, t : t + 1])
 
-        def negated_features(s):
+        def features(s):
             g, t = divmod(s, PACK)
             if s < len(FEATURES_AT):
-                neg_h = placed([P, S], F32, f"neg_h{s}", FEATURES_AT[s])
+                h_rows = placed([P, S], F32, f"h_rows{s}", FEATURES_AT[s])
             else:
-                neg_h = ring.tile([P, S], F32, name=f"neg_h{s}", tag="neg_h", bufs=SLICES - len(FEATURES_AT), align_bytes=64)
+                h_rows = ring.tile([P, S], F32, name=f"h_rows{s}", tag="h_rows", bufs=SLICES - len(FEATURES_AT), align_bytes=64)
             for half in range(HALVES):
                 cols = slice(half * BANK, (half + 1) * BANK)
                 acc = bank(f"h_acc{s}_{half}", "h_bank")
@@ -184,38 +184,24 @@ def tile_list_tilt_register_scores_kernel(
                         start=(a == 0),
                         stop=(a == PASSES1 - 1),
                     )
-                nc.scalar.activation(neg_h[:, cols], acc[:], ACT.Identity, bias=neg_bias[:, g, t : t + 1], scale=-1.0)
-            return neg_h
+                nc.scalar.activation(h_rows[:, cols], acc[:], ACT.Identity, bias=bias[:, g, t : t + 1])
+            return h_rows
 
-        def fetch_old(s):
-            old = ring.tile([P, S], F32, name=f"old{s}", tag="old", bufs=SLICES, align_bytes=64)
-            pieces = HALVES if s == 0 else 1
-            width = S // pieces
-            for i in range(pieces):
-                window = pages[s][:].indirect(entries(idx2, i * width, width))
-                nc.vector.tensor_copy(old[:, i * width : (i + 1) * width], window)
-            return old
+        excess = ring.tile([P, SLICES * S], F32, name="excess", align_bytes=64)
 
-        def rise_over(s, neg_h, old):
-            turned = placed([P, S], F32, f"turned{s}", TURNED_AT[s % len(TURNED_AT)])
-            rise = ring.tile([P, S], F32, name=f"rise{s}", tag="rise", bufs=2, align_bytes=64)
+        def relu(first, end):
+            nc.scalar.activation(excess[:, first:end], excess[:, first:end], ACT.Relu)
+
+        def fetch_excess(s, h_rows):
+            start = s * S
             for half in range(HALVES):
-                cols = slice(half * BANK, (half + 1) * BANK)
-                diff = bank(f"diff{s}_{half}", "d_bank")
-                for i in range(BANK // P):
-                    block = slice(half * BANK + i * P, half * BANK + (i + 1) * P)
-                    dst = diff[:, i * P : (i + 1) * P]
-                    nc.tensor.matmul(dst, lhsT=old[:, block], rhs=identity[:], is_transpose=True, start=True, stop=False)
-                    nc.tensor.matmul(dst, lhsT=neg_h[:, block], rhs=identity[:], is_transpose=True, start=False, stop=True)
-                nc.scalar.activation(turned[:, cols], diff[:], ACT.Relu, scale=-1.0)
-            for half in range(HALVES):
-                cols = slice(half * BANK, (half + 1) * BANK)
-                back = bank(f"back{s}_{half}", "r_bank")
-                for i in range(BANK // P):
-                    block = slice(half * BANK + i * P, half * BANK + (i + 1) * P)
-                    nc.tensor.transpose(back[:, i * P : (i + 1) * P], turned[:, block], identity[:])
-                nc.scalar.copy(rise[:, cols], back[:])
-            return rise
+                first = half * BANK
+                window = pages[s][:].indirect(entries(idx2, first, BANK))
+                dst = excess[:, start + first : start + first + BANK]
+                nc.vector.tensor_tensor(dst, window, h_rows[:, first : first + BANK], ALU.subtract)
+                if half == 0 and s > 0:
+                    relu(start - LINK, start + LINK)
+            relu(start + LINK if s > 0 else start, start + S - LINK if s < SLICES - 1 else start + S)
 
         def weave(engine_copy, dst, src):
             engine_copy(
@@ -231,7 +217,7 @@ def tile_list_tilt_register_scores_kernel(
         w_woven = []
 
         def weave_w2(g):
-            raw = placed([P, PACK, H], F32, f"w2_raw{g}", W2_AT)
+            raw = placed([P, PACK, H], F32, f"w2_raw{g}", W2_AT[g])
             nc.sync.dma_start(
                 out=raw[:], in_=w2[g * K_PASS : (g + 1) * K_PASS, :].rearrange("(p t) n -> p t n", t=PACK)
             )
@@ -245,7 +231,7 @@ def tile_list_tilt_register_scores_kernel(
             if g == 0:
                 codes = keep.tile([P, BANK], U32, name=name, align_bytes=64)
             else:
-                codes = placed([P, BANK], U32, name, TURNED_AT[SLICES % len(TURNED_AT)] + half * 2 * KB)
+                codes = placed([P, BANK], U32, name, SOIL_AT[1] + half * 2 * KB)
             plane = keep.tile([P, BANK], U8, name=f"w_plane{g}_{half}", align_bytes=64)
             woven = w_woven[g * (H // BANK) + half]
             nc.vector.quantize_mx(
@@ -260,13 +246,11 @@ def tile_list_tilt_register_scores_kernel(
             g, t = divmod(s, PACK)
             if t == 0:
                 x_rows.append(ring.tile([P, PACK, M], F32, name=f"x_rows{g}", tag="x_rows", bufs=1, align_bytes=64))
-            scaled = placed([P, M], F32, f"scaled_soil{s}", TURNED_AT[(s + 1) % len(TURNED_AT)] + KB)
-            nc.scalar.activation(scaled[:], soil_in[g][:, t, :], ACT.Copy, scale=gain[:, g, t : t + 1])
             width = M // pieces
             for i in range(pieces):
                 cols = slice(i * width, (i + 1) * width)
                 window = pages[s][:].indirect(entries(idx3, i * width, width))
-                nc.vector.tensor_tensor(x_rows[g][:, t, cols], window, scaled[:, cols], ALU.add)
+                nc.vector.tensor_tensor(x_rows[g][:, t, cols], window, soil_in[g][:, t, cols], ALU.add)
 
         y_acc = []
         x_codes = []
@@ -286,7 +270,7 @@ def tile_list_tilt_register_scores_kernel(
             x_codes.append(codes)
             x_planes.append(plane)
 
-        y_tags = 4 * ["h_bank"] + 2 * ["d_bank"] + 2 * ["r_bank"]
+        y_tags = (SLICES - HALVES) * ["y_bank"] + HALVES * ["h_bank"]
 
         def second_product(g):
             tiles_in_half = BANK // P
@@ -305,34 +289,29 @@ def tile_list_tilt_register_scores_kernel(
                     stop=(g == PASSES2 - 1),
                 )
 
-        olds = [fetch_old(0)]
-        rises = [rise_over(0, negated_features(0), olds[0])]
-        olds.append(fetch_old(1))
-        rises.append(rise_over(1, negated_features(1), olds[1]))
-        olds.append(fetch_old(2))
-        pages.append(load_page(3))
-        olds.append(fetch_old(3))
+        hs = [features(0)]
+        fetch_excess(0, hs[0])
         load_soil_in(0)
         soil_out = []
         for s in range(SLICES):
-            nc.vector.tensor_tensor(pages[s][:].indirect(idx2[:]), olds[s][:], rises[s][:], ALU.add)
+            if s + 1 < SLICES:
+                hs.append(features(s + 1))
+                fetch_excess(s + 1, hs[s + 1])
+            nc.vector.tensor_tensor(pages[s][:].indirect(idx2[:]), hs[s][:], excess[:, s * S : (s + 1) * S], ALU.add)
             if s > 0:
                 read_page(s - 1, 1)
-            if s + 2 < SLICES:
-                rises.append(rise_over(s + 2, negated_features(s + 2), olds[s + 2]))
-            if s + 4 < SLICES:
-                pages.append(load_page(s + 4))
-                olds.append(fetch_old(s + 4))
-            if s + 2 == len(FEATURES_AT) - 1:
-                weave_w2(0)
+            if s < 3:
+                pages.append(load_page(s + 5))
+            if s in (1, 2):
+                weave_w2(s - 1)
+            if s == 1:
                 quantize_w2(0, 0)
                 quantize_w2(0, 1)
-            if s - 1 == 2:
+            if s == 3:
                 load_soil_in(1)
-            if s - 1 == PACK - 1:
+            if s == PACK:
                 quantize_x(0, [nc.scalar.copy])
-                weave_w2(1)
-            if s + 2 == SLICES - 1:
+            if s + 1 == SLICES - 1:
                 second_product(0)
                 spent = ["v_words0_1", "v_words2_0", "v_words0_0", "v_words1_0", "v_words1_1", "v_words2_1"]
                 spent.extend(["rock_codes2", "rock_codes1"])

from contextlib import ExitStack

import concourse.mybir as mybir

K, H, T, S, T2, M = 1536, 1024, 4096, 1024, 2048, 512
FLOPS = 2 * K * H * S + 2 * H * H * M

F32 = mybir.dt.float32
BF16 = mybir.dt.bfloat16
I32 = mybir.dt.int32
U32 = mybir.dt.uint32
U16 = mybir.dt.uint16
U8 = mybir.dt.uint8
FP8X4 = mybir.dt.float8_e4m3fn_x4
FP4X4 = mybir.dt.float4_e2m1fn_x4
ALU = mybir.AluOpType
ACT = mybir.ActivationFunctionType

P = 128
PACK = 4
K_PASS = P * PACK
BANK = 512
QUADRANTS = 4
PASSES1 = K // K_PASS
PASSES2 = H // K_PASS
SLICES = H // P
HALVES = S // BANK
LINE = 16
LINK = 64
PLANE_ROWS = 32 * (QUADRANTS - 1) + 4

KB = 1024
TAB_AT = [15 * KB, 32 * KB, 0]
PICKED_SCALES_AT = 30 * KB
ROCK_SCALES_AT = 48 * KB
BIAS_AT = ROCK_SCALES_AT - 32
ROCK_AT = 56 * KB
TAB_SCALES_AT = 64 * KB
W2_AT = [68 * KB, 84 * KB]
PAGE_AT = [ROCK_AT, TAB_AT[1], TAB_AT[1] + 8 * KB, ROCK_SCALES_AT, TAB_AT[2], 16 * KB, ROCK_AT, TAB_AT[1]]
SOIL_AT = [TAB_AT[2] + 8 * KB, PAGE_AT[2]]
FEATURES_AT = [PAGE_AT[5], W2_AT[0], W2_AT[1]]


def tile_list_tilt_register_scores_kernel(
    tc, tab_words, tab_scales, offs, offs2, offs3, rock_words, rock_scales, b1, page0, soil, gs, w2, out
):
    nc = tc.nc
    with ExitStack() as ctx:
        lists = ctx.enter_context(tc.tile_pool(name="lists", bufs=1))
        keep = ctx.enter_context(tc.tile_pool(name="keep", bufs=1))
        ring = ctx.enter_context(tc.tile_pool(name="ring", bufs=1))
        arena = ctx.enter_context(tc.tile_pool(name="arena", bufs=1))
        psum = ctx.enter_context(tc.psum_pool(name="psum", bufs=1))

        def placed(shape, dtype, name, at):
            return arena.tile(shape, dtype, name=name, offset=at, align_bytes=64)

        def bank(name, tag):
            return psum.tile([P, BANK], F32, name=name, tag=tag, bufs=HALVES if tag == "h_bank" else SLICES - HALVES)

        def entries(offsets, first, count):
            return offsets[:, first // 16 : (first + count) // 16]

        idx = lists.tile([P, S // 16], U16, name="idx")
        idx2 = lists.tile([P, S // 16], U16, name="idx2")
        idx3 = lists.tile([P, M // 16], U16, name="idx3")

        tab_scale_rows = placed([P, T], U8, "tab_scale_rows", TAB_SCALES_AT)
        rock_scale_rows = placed([P, PASSES1, H], U8, "rock_scale_rows", ROCK_SCALES_AT)
        v_planes = [placed([P, S], U8, "v_plane0", PICKED_SCALES_AT)]
        v_planes.extend(keep.tile([P, S], U8, name=f"v_plane{a}", align_bytes=64) for a in range(1, PASSES1))
        nc.vector.memset(tab_scale_rows[:].bitcast(I32), 0)
        for a in range(1, PASSES1):
            nc.vector.memset(v_planes[a][:].bitcast(I32), 0)

        def load_table(a):
            words = placed([P, T], U32, f"tab{a}", TAB_AT[a])
            nc.sync.dma_start(
                out=words[:].bitcast(I32), in_=tab_words[a].rearrange("p t i -> p (t i)").bitcast(I32)
            )
            return words

        def load_page(s):
            g, t = divmod(s, PACK)
            page = placed([P, T2], F32, f"page{s}", PAGE_AT[s])
            rows = page0[g * K_PASS : (g + 1) * K_PASS, :].rearrange("(p t) c -> t p c", t=PACK)
            nc.sync.dma_start(out=page[:], in_=rows[t])
            return page

        bias_landing = arena.tile([P, PASSES2, 2 * PACK], F32, name="bias_landing", offset=BIAS_AT)
        nc.scalar.dma_start(out=bias_landing[:, :, 0:PACK], in_=b1.rearrange("(g p t) -> p g t", p=P, t=PACK))
        nc.sync.dma_start(idx[:], offs)
        nc.sync.dma_start(idx2[:], offs2)
        nc.sync.dma_start(idx3[:], offs3)
        gain = keep.tile([P, PASSES2, PACK], F32, name="gain")
        nc.scalar.dma_start(out=gain[:], in_=gs.rearrange("(g p t) -> p g t", p=P, t=PACK))
        bias = keep.tile([P, PASSES2, PACK], F32, name="bias")
        nc.scalar.copy(bias[:], bias_landing[:, :, 0:PACK])
        nc.gpsimd.memset(rock_scale_rows[:].bitcast(I32), 0)

        tabs = [load_table(0)]
        rock_raw = placed([P, PASSES1, 2 * H], U8, "rock_raw", ROCK_AT)
        nc.sync.dma_start(out=rock_raw[:].bitcast(I32), in_=rock_words.rearrange("a p c -> p a c").bitcast(I32))
        for q in range(QUADRANTS):
            nc.sync.dma_start(
                out=tab_scale_rows[32 * q : 32 * q + 4 * PASSES1, :].bitcast(I32),
                in_=tab_scales[:, 4 * q : 4 * q + 4, :].bitcast(I32),
            )
        tabs.append(load_table(1))
        for q in range(QUADRANTS):
            nc.sync.dma_start(
                out=rock_scale_rows[32 * q : 32 * q + 4, :, :].bitcast(I32),
                in_=rock_scales[:, 4 * q : 4 * q + 4, :].rearrange("a r c -> r a c").bitcast(I32),
            )

        def pick_words(a):
            picked = []
            for half in range(HALVES):
                name = f"v_words{a}_{half}"
                words = keep.tile([P, BANK], U32, name=name, tag=name, align_bytes=64)
                nc.vector.tensor_copy(words[:], tabs[a][:].indirect(entries(idx, half * BANK, BANK)))
                picked.append(words)
            return picked

        v_words = [pick_words(0)]
        tabs.append(load_table(2))
        nc.vector.tensor_copy(v_planes[0][:], tab_scale_rows[:].indirect(idx[:]))
        for a in range(1, PASSES1):
            nc.sync.dma_start(
                out=v_planes[a][0:PLANE_ROWS, :].bitcast(I32),
                in_=v_planes[0][4 * a : 4 * a + PLANE_ROWS, :].bitcast(I32),
            )

        rock_codes = []
        rock_planes = []
        for a in range(PASSES1):
            name = f"rock_codes{a}"
            if a == 0:
                codes = placed([P, 2 * H], U8, name, TAB_SCALES_AT)
            else:
                codes = keep.tile([P, 2 * H], U8, name=name, tag=name, align_bytes=64)
            nc.vector.tensor_copy(
                out=codes[:].bitcast(U16).rearrange("p (g t c q) -> p g c t q", g=PASSES2, t=PACK, q=LINE // 2),
                in_=rock_raw[:, a, :].bitcast(U16).rearrange("p (g c q t) -> p g c t q", g=PASSES2, t=PACK, q=LINE // 2),
            )
            rock_codes.append(codes)
            plane = keep.tile([P, H], U8, name=f"rock_plane{a}", align_bytes=64)
            nc.vector.tensor_copy(
                out=plane[:].rearrange("p (g t c q) -> p g c t q", g=PASSES2, t=PACK, q=LINE),
                in_=rock_scale_rows[:, a, :].rearrange("p (g c q t) -> p g c t q", g=PASSES2, t=PACK, q=LINE),
            )
            rock_planes.append(plane)
        v_words.extend(pick_words(a) for a in range(1, PASSES1))

        pages = [load_page(s) for s in range(5)]
        soil_in = []

        def load_soil_in(g):
            soil_in.append(placed([P, PACK, M], F32, f"soil_in{g}", SOIL_AT[g]))
            nc.sync.dma_start(
                out=soil_in[g][:], in_=soil[g * K_PASS : (g + 1) * K_PASS, :].rearrange("(p t) m -> p t m", t=PACK)
            )
            for t in range(PACK):
                rows = soil_in[g][:, t, :]
                nc.scalar.activation(rows, rows, ACT.Copy, scale=gain[:, g, t : t + 1])

        def features(s):
            g, t = divmod(s, PACK)
            if s < len(FEATURES_AT):
                h_rows = placed([P, S], F32, f"h_rows{s}", FEATURES_AT[s])
            else:
                h_rows = ring.tile([P, S], F32, name=f"h_rows{s}", tag="h_rows", bufs=SLICES - len(FEATURES_AT), align_bytes=64)
            for half in range(HALVES):
                cols = slice(half * BANK, (half + 1) * BANK)
                acc = bank(f"h_acc{s}_{half}", "h_bank")
                for a in range(PASSES1):
                    nc.tensor.matmul_mx(
                        out=acc[:],
                        lhsT=rock_codes[a][:, 2 * P * s : 2 * P * (s + 1)].bitcast(FP4X4),
                        lhsT_scale=rock_planes[a][:, P * s : P * (s + 1)],
                        rhs=v_words[a][half][:].bitcast(FP8X4),
                        rhs_scale=v_planes[a][:, cols],
                        start=(a == 0),
                        stop=(a == PASSES1 - 1),
                    )
                nc.scalar.activation(h_rows[:, cols], acc[:], ACT.Identity, bias=bias[:, g, t : t + 1])
            return h_rows

        excess = ring.tile([P, SLICES * S], F32, name="excess", align_bytes=64)

        def relu(first, end):
            nc.scalar.activation(excess[:, first:end], excess[:, first:end], ACT.Relu)

        def fetch_excess(s, h_rows):
            start = s * S
            for half in range(HALVES):
                first = half * BANK
                window = pages[s][:].indirect(entries(idx2, first, BANK))
                dst = excess[:, start + first : start + first + BANK]
                nc.vector.tensor_tensor(dst, window, h_rows[:, first : first + BANK], ALU.subtract)
                if half == 0 and s > 0:
                    relu(start - LINK, start + LINK)
            relu(start + LINK if s > 0 else start, start + S - LINK if s < SLICES - 1 else start + S)

        def weave(engine_copy, dst, src):
            engine_copy(
                out=dst.rearrange("p (c i) t -> p c t i", i=LINE // 4),
                in_=src.rearrange("p t (c i) -> p c t i", i=LINE // 4),
            )

        def woven_tile(name):
            return ring.tile([P, BANK, PACK], BF16, name=name, tag="woven", bufs=3, align_bytes=64)

        w_codes = []
        w_planes = []
        w_woven = []

        def weave_w2(g):
            raw = placed([P, PACK, H], F32, f"w2_raw{g}", W2_AT[g])
            nc.sync.dma_start(
                out=raw[:], in_=w2[g * K_PASS : (g + 1) * K_PASS, :].rearrange("(p t) n -> p t n", t=PACK)
            )
            for half in range(H // BANK):
                woven = woven_tile(f"w2_woven{g}_{half}")
                weave(nc.scalar.copy, woven[:], raw[:, :, half * BANK : (half + 1) * BANK])
                w_woven.append(woven)

        def quantize_w2(g, half):
            name = f"w_codes{g}_{half}"
            if g == 0:
                codes = keep.tile([P, BANK], U32, name=name, align_bytes=64)
            else:
                codes = placed([P, BANK], U32, name, SOIL_AT[1] + half * 2 * KB)
            plane = keep.tile([P, BANK], U8, name=f"w_plane{g}_{half}", align_bytes=64)
            woven = w_woven[g * (H // BANK) + half]
            nc.vector.quantize_mx(
                out=codes[:].bitcast(FP8X4), scales=plane[:], in_=woven[:].rearrange("p c t -> p (c t)")
            )
            w_codes.append(codes)
            w_planes.append(plane)

        x_rows = []

        def read_page(s, pieces):
            g, t = divmod(s, PACK)
            if t == 0:
                x_rows.append(ring.tile([P, PACK, M], F32, name=f"x_rows{g}", tag="x_rows", bufs=1, align_bytes=64))
            width = M // pieces
            for i in range(pieces):
                cols = slice(i * width, (i + 1) * width)
                window = pages[s][:].indirect(entries(idx3, i * width, width))
                nc.vector.tensor_tensor(x_rows[g][:, t, cols], window, soil_in[g][:, t, cols], ALU.add)

        y_acc = []
        x_codes = []
        x_planes = []

        def quantize_x(g, copies):
            woven = woven_tile(f"x_woven{g}")
            width = M // len(copies)
            for i, engine_copy in enumerate(copies):
                cols = slice(i * width, (i + 1) * width)
                weave(engine_copy, woven[:, cols, :], x_rows[g][:, :, cols])
            codes = keep.tile([P, M], U32, name=f"x_codes{g}", align_bytes=64)
            plane = keep.tile([P, M], U8, name=f"x_plane{g}", align_bytes=64)
            nc.vector.quantize_mx(
                out=codes[:].bitcast(FP8X4), scales=plane[:], in_=woven[:].rearrange("p c t -> p (c t)")
            )
            x_codes.append(codes)
            x_planes.append(plane)

        y_tags = (SLICES - HALVES) * ["y_bank"] + HALVES * ["h_bank"]

        def second_product(g):
            tiles_in_half = BANK // P
            for n in range(SLICES):
                if g == 0:
                    y_acc.append(bank(f"y_acc{n}", y_tags[n]))
                which = g * (H // BANK) + n // tiles_in_half
                cols = slice((n % tiles_in_half) * P, (n % tiles_in_half + 1) * P)
                nc.tensor.matmul_mx(
                    out=y_acc[n][:],
                    lhsT=w_codes[which][:, cols].bitcast(FP8X4),
                    lhsT_scale=w_planes[which][:, cols],
                    rhs=x_codes[g][:].bitcast(FP8X4),
                    rhs_scale=x_planes[g][:],
                    start=(g == 0),
                    stop=(g == PASSES2 - 1),
                )

        hs = [features(0)]
        fetch_excess(0, hs[0])
        load_soil_in(0)
        soil_out = []
        for s in range(SLICES):
            if s + 1 < SLICES:
                hs.append(features(s + 1))
                fetch_excess(s + 1, hs[s + 1])
            nc.vector.tensor_tensor(pages[s][:].indirect(idx2[:]), hs[s][:], excess[:, s * S : (s + 1) * S], ALU.add)
            if s > 0:
                read_page(s - 1, 1)
            if s < 3:
                pages.append(load_page(s + 5))
            if s in (1, 2):
                weave_w2(s - 1)
            if s == 1:
                quantize_w2(0, 0)
                quantize_w2(0, 1)
            if s == 3:
                load_soil_in(1)
            if s == PACK:
                quantize_x(0, [nc.scalar.copy])
            if s + 1 == SLICES - 1:
                second_product(0)
                spent = ["v_words0_1", "v_words2_0", "v_words0_0", "v_words1_0", "v_words1_1", "v_words2_1"]
                spent.extend(["rock_codes2", "rock_codes1"])
                for n in range(SLICES):
                    soil_out.append(keep.tile([P, M], F32, name=f"soil_out{n}", tag=spent[n], align_bytes=64))
                    nc.sync.dma_start(out=soil_out[n][:], in_=soil[n * P : (n + 1) * P, :])
        read_page(SLICES - 1, 2)
        quantize_w2(1, 0)
        quantize_x(1, [nc.scalar.copy, nc.vector.tensor_copy])
        quantize_w2(1, 1)
        second_product(1)

        for n in range(SLICES):
            pieces = 2 if n == SLICES - 1 else 1
            width = M // pieces
            for i in range(pieces):
                cols = slice(i * width, (i + 1) * width)
                z = soil_out[n][:, cols]
                nc.vector.tensor_tensor(z, y_acc[n][:, cols], z, ALU.add)
                nc.scalar.activation(z, z, ACT.Sigmoid)
                nc.sync.dma_start(out=out[n * P : (n + 1) * P, cols], in_=z)
